import numpy as np
import ml_dtypes


def mxq(x, axis, fmt="e4m3"):
    dtype, down = {"e4m3": (ml_dtypes.float8_e4m3fn, 7), "e5m2": (ml_dtypes.float8_e5m2, 14)}[fmt]
    v = np.moveaxis(np.asarray(x, np.float32).astype(ml_dtypes.bfloat16).astype(np.float64), axis, -1)
    blocks = v.reshape(v.shape[:-1] + (-1, 32))
    amax = np.abs(blocks).max(-1, keepdims=True)
    byte = np.maximum(np.where(amax > 0, np.frexp(amax)[1] - 1 + 127, 0) - down, 1)
    scale = np.exp2(byte - 127.0)
    codes = (blocks / scale).astype(np.float32).astype(dtype).astype(np.float64)
    return np.moveaxis((codes * scale).reshape(v.shape), -1, axis)


WIDE = False


def mx_kscale(k):
    if not WIDE:
        return np.ones(k)
    levels = np.array([10, -10, 5, -5, 0])
    if k % 512:
        return np.exp2(np.random.permutation(np.resize(levels, k // 32))).repeat(32)
    a = np.empty((k // 512, 16))
    for p in range(k // 512):
        a[p, :8] = np.random.permutation(np.resize(levels, 8))
        for g in range(8):
            far = levels[np.abs(levels - a[p, g]) >= 10]
            a[p, g + 8] = far[np.random.randint(len(far))]
    return np.exp2(a.ravel()).repeat(32)


def f64(x):
    return np.asarray(x).astype(np.float64)


def striped(idx):
    return np.tile(idx.reshape(-1, 16).T, (8, 1)).astype(np.uint16)


def unstriped(offs):
    return offs[:16].T.reshape(-1).astype(np.int64)


def pack_weight(w):
    k, n = w.shape
    w = f64(np.asarray(w, np.float32).astype(ml_dtypes.bfloat16)).reshape(k // 32, 32, n)
    amax = np.abs(w).max(1)
    byte = np.clip(np.where(amax > 0, np.frexp(amax)[1] - 1 + 127 - 7, 1), 1, 254)
    scaled = (w * np.exp2(127.0 - byte)[:, None, :]).reshape(k, n).astype(np.float32)
    words = np.ascontiguousarray(scaled.reshape(k // 512, 128, 4, n).transpose(0, 1, 3, 2)).astype(ml_dtypes.float8_e4m3fn).view(np.uint8)
    return words, np.ascontiguousarray(byte.astype(np.uint8).reshape(k // 512, 16, n))


def unpack_weight(words, scales):
    g, p, n, _ = words.shape
    vals = np.ascontiguousarray(words).view(ml_dtypes.float8_e4m3fn).astype(np.float64) * np.repeat(np.exp2(scales.astype(np.float64) - 127.0), 8, axis=1)[..., None]
    return vals.transpose(0, 1, 3, 2).reshape(g * 512, n)


K, T, S, H, N = 512, 2048, 512, 512, 256
P = 2 ** 7


def setup_inputs():
    n = np.random.standard_normal
    s = mx_kscale(K)[:, None]
    u = mx_kscale(H)
    packed_xT = pack_weight(n((K, T)) * s)
    return {
        "x_words": packed_xT[0],
        "x_scales": packed_xT[1],
        "w1": (n((K, H)) / np.sqrt(K) / s * u).astype(np.float32),
        "w2": (n((H, N)) / np.sqrt(H) / u[:, None]).astype(np.float32),
        "eq": (n((H, S)) * u[:, None]).astype(np.float32),
        "rate": (np.random.uniform(0.2, 1.8, (H, 1))).astype(np.float32),
        "thru": (np.tile(np.random.uniform(0.3, 1.0, S), (P, 1))).astype(np.float32),
        "shut": (np.tile(np.random.uniform(0.0, 0.7, S), (P, 1))).astype(np.float32),
        "offs": striped(np.random.permutation(T)[:S]),
        "src": striped(np.random.permutation(S)),
    }


def reference(x_words, x_scales, w1, w2, eq, rate, thru, shut, offs, src):
    xq = unpack_weight(x_words, x_scales)[:, unstriped(offs)]
    y = mxq(f64(w1), 0, "e4m3").T @ xq
    rr = y + f64(rate) * (f64(eq) - y)
    f = mxq(f64(w2), 0, "e4m3").T @ mxq(rr, 0, "e4m3")
    return f[:, unstriped(src)] * f64(thru)[:1] + f * f64(shut)[:1]

@@ -1,0 +1,142 @@
+from contextlib import ExitStack
+
+import concourse.mybir as mybir
+
+K, T, S, H, N = 512, 2048, 512, 512, 256
+FLOPS = 2 * K * H * S + 2 * H * N * S
+
+F32 = mybir.dt.float32
+BF16 = mybir.dt.bfloat16
+I32 = mybir.dt.int32
+U32 = mybir.dt.uint32
+U16 = mybir.dt.uint16
+U8 = mybir.dt.uint8
+FP8X4 = mybir.dt.float8_e4m3fn_x4
+MULT = mybir.AluOpType.mult
+ADD = mybir.AluOpType.add
+COPY = mybir.ActivationFunctionType.Copy
+
+P = 128
+PACK = 4
+HALF = S // 2
+LIST_COLS = HALF // 16
+
+
+def tile_picked_ylbm_part_p_kernel(tc, x_words, x_scales, w1, w2, eq, rate, thru, shut, offs, src, out):
+    nc = tc.nc
+    with ExitStack() as ctx:
+        keep = ctx.enter_context(tc.tile_pool(name="keep", bufs=1))
+        psum = ctx.enter_context(tc.psum_pool(name="psum", bufs=8))
+
+        offs_sb = keep.tile([P, S // 16], U16, name="offs_sb")
+        src_sb = keep.tile([P, S // 16], U16, name="src_sb")
+        xw = keep.tile([P, T], U32, name="xw", align_bytes=64)
+        xs = keep.tile([P, T], U8, name="xs", align_bytes=64)
+        w1_raw = [keep.tile([P, PACK, HALF], F32, name="w1_raw%d" % h) for h in range(2)]
+        w2_raw = keep.tile([P, PACK, N], F32, name="w2_raw")
+        eq_sb = [keep.tile([P, PACK, HALF], F32, name="eq%d" % h) for h in range(2)]
+        rate_sb = keep.tile([P, PACK], F32, name="rate_sb")
+        keep_sb = keep.tile([P, PACK], F32, name="keep_sb")
+        thru_sb = keep.tile([P, S], F32, name="thru_sb")
+        shut_sb = keep.tile([P, S], F32, name="shut_sb")
+
+        nc.vector.memset(xs[:].bitcast(I32), 0)
+
+        w1_rows = w1.rearrange("(p j) c -> p j c", j=PACK)
+        eq_rows = eq.rearrange("(p t) c -> p t c", t=PACK)
+        nc.sync.dma_start(offs_sb[:], offs)
+        nc.sync.dma_start(w1_raw[0][:], w1_rows[:, :, 0:HALF])
+        for q in range(4):
+            nc.sync.dma_start(xs[32 * q : 32 * q + 4, :].bitcast(I32), x_scales[0, 4 * q : 4 * q + 4, :].bitcast(I32))
+        nc.sync.dma_start(w1_raw[1][:], w1_rows[:, :, HALF : 2 * HALF])
+        nc.sync.dma_start(xw[:].bitcast(I32), x_words[0].rearrange("p c r -> p (c r)").bitcast(I32))
+        nc.sync.dma_start(rate_sb[:], rate.rearrange("(p t) o -> p (t o)", t=PACK))
+        nc.sync.dma_start(eq_sb[0][:], eq_rows[:, :, 0:HALF])
+        nc.sync.dma_start(w2_raw[:], w2.rearrange("(p j) c -> p j c", j=PACK))
+        nc.sync.dma_start(eq_sb[1][:], eq_rows[:, :, HALF : 2 * HALF])
+        nc.sync.dma_start(shut_sb[:], shut)
+        nc.sync.dma_start(thru_sb[:], thru)
+        nc.sync.dma_start(src_sb[:], src)
+
+        w1_bf = keep.tile([P, PACK, P, PACK], BF16, name="w1_bf", align_bytes=64)
+        MH = P // 2
+        nc.scalar.activation(
+            w1_bf[:, :, 0:MH, :].rearrange("p t m j -> p m j t"),
+            w1_raw[0][:].rearrange("p j (m t) -> p m j t", t=PACK), COPY)
+        xs_g = keep.tile([P, S], U8, name="xs_g", align_bytes=64)
+        nc.vector.tensor_copy(xs_g[:], xs[:].indirect(offs_sb[:]))
+        nc.vector.tensor_copy(
+            w1_bf[:, :, MH:P, :].rearrange("p t m j -> p m j t"),
+            w1_raw[1][:].rearrange("p j (m t) -> p m j t", t=PACK))
+        w1_codes = keep.tile([P, H], U32, name="w1_codes", align_bytes=64)
+        w1_sc = keep.tile([P, H], U8, name="w1_sc", align_bytes=64)
+        nc.vector.quantize_mx(out=w1_codes[:].bitcast(FP8X4), scales=w1_sc[:], in_=w1_bf[:].rearrange("p t m j -> p (t m j)"))
+        nc.vector.tensor_scalar(keep_sb[:], rate_sb[:], -1.0, 1.0, MULT, ADD)
+
+        xw_g = [keep.tile([P, HALF], U32, name="xw_g%d" % h, align_bytes=64) for h in range(2)]
+        for h in range(2):
+            nc.vector.tensor_copy(xw_g[h][:], xw[:].indirect(offs_sb[:, h * LIST_COLS : (h + 1) * LIST_COLS]))
+
+        kept = {}
+        for h in range(2):
+            for t in range(PACK):
+                y = psum.tile([P, HALF], F32, name="acc")
+                nc.tensor.matmul_mx(out=y[:], lhsT=w1_codes[:, t * P : (t + 1) * P].bitcast(FP8X4),
+                                    lhsT_scale=w1_sc[:, t * P : (t + 1) * P],
+                                    rhs=xw_g[h][:].bitcast(FP8X4), rhs_scale=xs_g[:, h * HALF : (h + 1) * HALF],
+                                    start=True, stop=True)
+                kept[h, t] = keep.tile([P, HALF], F32, name="kept%d%d" % (h, t))
+                nc.scalar.activation(kept[h, t][:], y[:], COPY, scale=keep_sb[:, t : t + 1])
+
+        rr_pl = [keep.tile([P, PACK, HALF], BF16, name="rr_pl%d" % h) for h in range(2)]
+        rr_bf = [keep.tile([P, HALF, PACK], BF16, name="rr_bf%d" % h, align_bytes=64) for h in range(2)]
+        rr_codes = [keep.tile([P, HALF], U32, name="rr_codes%d" % h, align_bytes=64) for h in range(2)]
+        rr_sc = [keep.tile([P, HALF], U8, name="rr_sc%d" % h, align_bytes=64) for h in range(2)]
+
+        def relax(h):
+            for t in range(PACK):
+                nc.vector.scalar_tensor_tensor(rr_pl[h][:, t, :], eq_sb[h][:, t, :], rate_sb[:, t : t + 1], kept[h, t][:], MULT, ADD)
+
+        def weave_views(h):
+            return (rr_bf[h][:].rearrange("p (c i) t -> p c t i", i=4), rr_pl[h][:].rearrange("p t (c i) -> p c t i", i=4))
+
+        def quant_rr(h):
+            nc.vector.quantize_mx(out=rr_codes[h][:].bitcast(FP8X4), scales=rr_sc[h][:], in_=rr_bf[h][:].rearrange("p c t -> p (c t)"))
+
+        relax(0)
+        w2_bf = keep.tile([P, N, PACK], BF16, name="w2_bf", align_bytes=64)
+        nc.vector.tensor_copy(w2_bf[:].rearrange("p (c i) j -> p c j i", i=4), w2_raw[:].rearrange("p j (c i) -> p c j i", i=4))
+        o, i = weave_views(0)
+        nc.scalar.copy(o, i)
+        relax(1)
+        w2_codes = keep.tile([P, N], U32, name="w2_codes", align_bytes=64)
+        w2_sc = keep.tile([P, N], U8, name="w2_sc", align_bytes=64)
+        nc.vector.quantize_mx(out=w2_codes[:].bitcast(FP8X4), scales=w2_sc[:], in_=w2_bf[:].rearrange("p c j -> p (c j)"))
+        o, i = weave_views(1)
+        nc.vector.tensor_copy(o, i)
+        quant_rr(0)
+        quant_rr(1)
+
+        f_sb = [keep.tile([P, S], F32, name="f_sb%d" % m) for m in range(2)]
+        own = [keep.tile([P, S], F32, name="own%d" % m) for m in range(2)]
+        for h in range(2):
+            cols = slice(h * HALF, (h + 1) * HALF)
+            for m in range(2):
+                f = psum.tile([P, HALF], F32, name="acc")
+                nc.tensor.matmul_mx(out=f[:], lhsT=w2_codes[:, m * P : (m + 1) * P].bitcast(FP8X4),
+                                    lhsT_scale=w2_sc[:, m * P : (m + 1) * P],
+                                    rhs=rr_codes[h][:].bitcast(FP8X4), rhs_scale=rr_sc[h][:], start=True, stop=True)
+                nc.scalar.copy(f_sb[m][:, cols], f[:])
+                nc.vector.tensor_tensor(own[m][:, cols], f_sb[m][:, cols], shut_sb[:, cols], MULT)
+
+        for m in range(2):
+            got = {}
+            for h in range(2):
+                cols = slice(h * HALF, (h + 1) * HALF)
+                got[h] = keep.tile([P, HALF], F32, name="got%d%d" % (m, h))
+                nc.vector.tensor_tensor(got[h][:], f_sb[m][:].indirect(src_sb[:, h * LIST_COLS : (h + 1) * LIST_COLS]), thru_sb[:, cols], MULT)
+            for h in range(2):
+                cols = slice(h * HALF, (h + 1) * HALF)
+                res = keep.tile([P, HALF], F32, name="res%d%d" % (m, h))
+                nc.vector.tensor_tensor(res[:], got[h][:], own[m][:, cols], ADD)
+                nc.sync.dma_start(out[m * P : (m + 1) * P, cols], res[:])

@@ -1,6 +1,7 @@
 from contextlib import ExitStack
 
 import concourse.mybir as mybir
+from concourse.masks import make_identity
 
 K, T, S, H, N = 512, 2048, 512, 512, 256
 FLOPS = 2 * K * H * S + 2 * H * N * S
@@ -32,111 +33,139 @@ def tile_picked_ylbm_part_p_kernel(tc, x_words, x_scales, w1, w2, eq, rate, thru
         src_sb = keep.tile([P, S // 16], U16, name="src_sb")
         xw = keep.tile([P, T], U32, name="xw", align_bytes=64)
         xs = keep.tile([P, T], U8, name="xs", align_bytes=64)
-        w1_raw = [keep.tile([P, PACK, HALF], F32, name="w1_raw%d" % h) for h in range(2)]
+        w1_raw = keep.tile([P, PACK, H], F32, name="w1_raw")
         w2_raw = keep.tile([P, PACK, N], F32, name="w2_raw")
-        eq_sb = [keep.tile([P, PACK, HALF], F32, name="eq%d" % h) for h in range(2)]
+        eq_sb = [keep.tile([P, 2, S], F32, name="eq%d" % u) for u in range(2)]
         rate_sb = keep.tile([P, PACK], F32, name="rate_sb")
         keep_sb = keep.tile([P, PACK], F32, name="keep_sb")
         thru_sb = keep.tile([P, S], F32, name="thru_sb")
-        shut_sb = keep.tile([P, S], F32, name="shut_sb")
+        shut_t = keep.tile([P, S // P], F32, name="shut_t")
+        ident = keep.tile([P, P], F32, name="ident")
 
         nc.vector.memset(xs[:].bitcast(I32), 0)
+        nc.gpsimd.dma_start(rate_sb[:], rate.rearrange("(p t) o -> p (t o)", t=PACK))
+        make_identity(nc, ident[:])
+        nc.scalar.activation(keep_sb[:], rate_sb[:], COPY, scale=-1.0, bias=1.0)
 
-        w1_rows = w1.rearrange("(p j) c -> p j c", j=PACK)
         eq_rows = eq.rearrange("(p t) c -> p t c", t=PACK)
+        w1_rows = w1.rearrange("(p j) c -> p j c", j=PACK)
+        nc.sync.dma_start(w1_raw[:, 0:2, :], w1_rows[:, 0:2, :])
         nc.sync.dma_start(offs_sb[:], offs)
-        nc.sync.dma_start(w1_raw[0][:], w1_rows[:, :, 0:HALF])
         for q in range(4):
             nc.sync.dma_start(xs[32 * q : 32 * q + 4, :].bitcast(I32), x_scales[0, 4 * q : 4 * q + 4, :].bitcast(I32))
-        nc.sync.dma_start(w1_raw[1][:], w1_rows[:, :, HALF : 2 * HALF])
+        nc.sync.dma_start(w1_raw[:, 2:4, :], w1_rows[:, 2:4, :])
         nc.sync.dma_start(xw[:].bitcast(I32), x_words[0].rearrange("p c r -> p (c r)").bitcast(I32))
-        nc.sync.dma_start(rate_sb[:], rate.rearrange("(p t) o -> p (t o)", t=PACK))
-        nc.sync.dma_start(eq_sb[0][:], eq_rows[:, :, 0:HALF])
         nc.sync.dma_start(w2_raw[:], w2.rearrange("(p j) c -> p j c", j=PACK))
-        nc.sync.dma_start(eq_sb[1][:], eq_rows[:, :, HALF : 2 * HALF])
-        nc.sync.dma_start(shut_sb[:], shut)
+        for u in range(2):
+            nc.sync.dma_start(eq_sb[u][:], eq_rows[:, 2 * u : 2 * u + 2, :])
         nc.sync.dma_start(thru_sb[:], thru)
         nc.sync.dma_start(src_sb[:], src)
+        with nc.allow_non_contiguous_dma(reason="one value of shut to a partition"):
+            nc.sync.dma_start(shut_t[:], shut[0].rearrange("(b p) -> p b", p=P))
 
-        w1_bf = keep.tile([P, PACK, P, PACK], BF16, name="w1_bf", align_bytes=64)
-        MH = P // 2
-        nc.scalar.activation(
-            w1_bf[:, :, 0:MH, :].rearrange("p t m j -> p m j t"),
-            w1_raw[0][:].rearrange("p j (m t) -> p m j t", t=PACK), COPY)
         xs_g = keep.tile([P, S], U8, name="xs_g", align_bytes=64)
         nc.vector.tensor_copy(xs_g[:], xs[:].indirect(offs_sb[:]))
-        nc.vector.tensor_copy(
-            w1_bf[:, :, MH:P, :].rearrange("p t m j -> p m j t"),
-            w1_raw[1][:].rearrange("p j (m t) -> p m j t", t=PACK))
-        w1_codes = keep.tile([P, H], U32, name="w1_codes", align_bytes=64)
-        w1_sc = keep.tile([P, H], U8, name="w1_sc", align_bytes=64)
-        nc.vector.quantize_mx(out=w1_codes[:].bitcast(FP8X4), scales=w1_sc[:], in_=w1_bf[:].rearrange("p t m j -> p (t m j)"))
-        nc.vector.tensor_scalar(keep_sb[:], rate_sb[:], -1.0, 1.0, MULT, ADD)
+
+        w1_bf = [keep.tile([P, 2, P, PACK], BF16, name="w1_bf%d" % u, align_bytes=64) for u in range(2)]
+        w1_codes = [keep.tile([P, 2, P], U32, name="w1_codes%d" % u, align_bytes=64) for u in range(2)]
+        w1_sc = [keep.tile([P, 2, P], U8, name="w1_sc%d" % u, align_bytes=64) for u in range(2)]
+
+        def w1_views(u):
+            return (w1_bf[u][:].rearrange("p t m j -> p m j t"),
+                    w1_raw[:].rearrange("p j (m t) -> p m j t", t=PACK)[:, :, :, 2 * u : 2 * u + 2])
+
+        o, i = w1_views(0)
+        nc.vector.tensor_copy(o, i)
+        o, i = w1_views(1)
+        nc.scalar.activation(o, i, COPY)
+        for u in range(2):
+            nc.vector.quantize_mx(out=w1_codes[u][:].rearrange("p t m -> p (t m)").bitcast(FP8X4), scales=w1_sc[u][:].rearrange("p t m -> p (t m)"),
+                                  in_=w1_bf[u][:].rearrange("p t m j -> p (t m j)"))
 
         xw_g = [keep.tile([P, HALF], U32, name="xw_g%d" % h, align_bytes=64) for h in range(2)]
         for h in range(2):
             nc.vector.tensor_copy(xw_g[h][:], xw[:].indirect(offs_sb[:, h * LIST_COLS : (h + 1) * LIST_COLS]))
 
         kept = {}
-        for h in range(2):
-            for t in range(PACK):
-                y = psum.tile([P, HALF], F32, name="acc")
-                nc.tensor.matmul_mx(out=y[:], lhsT=w1_codes[:, t * P : (t + 1) * P].bitcast(FP8X4),
-                                    lhsT_scale=w1_sc[:, t * P : (t + 1) * P],
-                                    rhs=xw_g[h][:].bitcast(FP8X4), rhs_scale=xs_g[:, h * HALF : (h + 1) * HALF],
-                                    start=True, stop=True)
-                kept[h, t] = keep.tile([P, HALF], F32, name="kept%d%d" % (h, t))
-                nc.scalar.activation(kept[h, t][:], y[:], COPY, scale=keep_sb[:, t : t + 1])
+        for u in range(2):
+            for h in range(2):
+                for e in range(2):
+                    t = 2 * u + e
+                    y = psum.tile([P, HALF], F32, name="acc")
+                    nc.tensor.matmul_mx(out=y[:], lhsT=w1_codes[u][:, e, :].bitcast(FP8X4), lhsT_scale=w1_sc[u][:, e, :],
+                                        rhs=xw_g[h][:].bitcast(FP8X4), rhs_scale=xs_g[:, h * HALF : (h + 1) * HALF],
+                                        start=True, stop=True)
+                    kept[h, t] = keep.tile([P, HALF], F32, name="kept%d%d" % (h, t))
+                    nc.scalar.activation(kept[h, t][:], y[:], COPY, scale=keep_sb[:, t : t + 1])
+
+        w2_bf = keep.tile([P, N, PACK], BF16, name="w2_bf", align_bytes=64)
+        nc.vector.tensor_copy(w2_bf[:].rearrange("p (c i) j -> p c j i", i=4), w2_raw[:].rearrange("p j (c i) -> p c j i", i=4))
+        w2_codes = keep.tile([P, N], U32, name="w2_codes", align_bytes=64)
+        w2_sc = keep.tile([P, N], U8, name="w2_sc", align_bytes=64)
+        nc.vector.quantize_mx(out=w2_codes[:].bitcast(FP8X4), scales=w2_sc[:], in_=w2_bf[:].rearrange("p c j -> p (c j)"))
 
         rr_pl = [keep.tile([P, PACK, HALF], BF16, name="rr_pl%d" % h) for h in range(2)]
         rr_bf = [keep.tile([P, HALF, PACK], BF16, name="rr_bf%d" % h, align_bytes=64) for h in range(2)]
-        rr_codes = [keep.tile([P, HALF], U32, name="rr_codes%d" % h, align_bytes=64) for h in range(2)]
-        rr_sc = [keep.tile([P, HALF], U8, name="rr_sc%d" % h, align_bytes=64) for h in range(2)]
+        rr_codes = keep.tile([P, S], U32, name="rr_codes", align_bytes=64)
+        rr_sc = keep.tile([P, S], U8, name="rr_sc", align_bytes=64)
 
-        def relax(h):
-            for t in range(PACK):
-                nc.vector.scalar_tensor_tensor(rr_pl[h][:, t, :], eq_sb[h][:, t, :], rate_sb[:, t : t + 1], kept[h, t][:], MULT, ADD)
+        for u in range(2):
+            for h in range(2):
+                for e in range(2):
+                    t = 2 * u + e
+                    nc.vector.scalar_tensor_tensor(rr_pl[h][:, t, :], eq_sb[u][:, e, h * HALF : (h + 1) * HALF], rate_sb[:, t : t + 1], kept[h, t][:], MULT, ADD)
 
         def weave_views(h):
             return (rr_bf[h][:].rearrange("p (c i) t -> p c t i", i=4), rr_pl[h][:].rearrange("p t (c i) -> p c t i", i=4))
 
-        def quant_rr(h):
-            nc.vector.quantize_mx(out=rr_codes[h][:].bitcast(FP8X4), scales=rr_sc[h][:], in_=rr_bf[h][:].rearrange("p c t -> p (c t)"))
-
-        relax(0)
-        w2_bf = keep.tile([P, N, PACK], BF16, name="w2_bf", align_bytes=64)
-        nc.vector.tensor_copy(w2_bf[:].rearrange("p (c i) j -> p c j i", i=4), w2_raw[:].rearrange("p j (c i) -> p c j i", i=4))
         o, i = weave_views(0)
         nc.scalar.copy(o, i)
-        relax(1)
-        w2_codes = keep.tile([P, N], U32, name="w2_codes", align_bytes=64)
-        w2_sc = keep.tile([P, N], U8, name="w2_sc", align_bytes=64)
-        nc.vector.quantize_mx(out=w2_codes[:].bitcast(FP8X4), scales=w2_sc[:], in_=w2_bf[:].rearrange("p c j -> p (c j)"))
         o, i = weave_views(1)
         nc.vector.tensor_copy(o, i)
-        quant_rr(0)
-        quant_rr(1)
+        for h in range(2):
+            nc.vector.quantize_mx(out=rr_codes[:, h * HALF : (h + 1) * HALF].bitcast(FP8X4), scales=rr_sc[:, h * HALF : (h + 1) * HALF], in_=rr_bf[h][:].rearrange("p c t -> p (c t)"))
 
         f_sb = [keep.tile([P, S], F32, name="f_sb%d" % m) for m in range(2)]
-        own = [keep.tile([P, S], F32, name="own%d" % m) for m in range(2)]
-        for h in range(2):
-            cols = slice(h * HALF, (h + 1) * HALF)
-            for m in range(2):
-                f = psum.tile([P, HALF], F32, name="acc")
+        for m, width in ((0, HALF), (1, S)):
+            for c0 in range(0, S, width):
+                cols = slice(c0, c0 + width)
+                f = psum.tile([P, width], F32, name="acc")
                 nc.tensor.matmul_mx(out=f[:], lhsT=w2_codes[:, m * P : (m + 1) * P].bitcast(FP8X4),
                                     lhsT_scale=w2_sc[:, m * P : (m + 1) * P],
-                                    rhs=rr_codes[h][:].bitcast(FP8X4), rhs_scale=rr_sc[h][:], start=True, stop=True)
+                                    rhs=rr_codes[:, cols].bitcast(FP8X4), rhs_scale=rr_sc[:, cols], start=True, stop=True)
                 nc.scalar.copy(f_sb[m][:, cols], f[:])
-                nc.vector.tensor_tensor(own[m][:, cols], f_sb[m][:, cols], shut_sb[:, cols], MULT)
 
-        for m in range(2):
-            got = {}
-            for h in range(2):
-                cols = slice(h * HALF, (h + 1) * HALF)
-                got[h] = keep.tile([P, HALF], F32, name="got%d%d" % (m, h))
-                nc.vector.tensor_tensor(got[h][:], f_sb[m][:].indirect(src_sb[:, h * LIST_COLS : (h + 1) * LIST_COLS]), thru_sb[:, cols], MULT)
-            for h in range(2):
-                cols = slice(h * HALF, (h + 1) * HALF)
-                res = keep.tile([P, HALF], F32, name="res%d%d" % (m, h))
-                nc.vector.tensor_tensor(res[:], got[h][:], own[m][:, cols], ADD)
-                nc.sync.dma_start(out[m * P : (m + 1) * P, cols], res[:])
+        own_t = {}
+        for b in range(S // P):
+            f_t = psum.tile([P, 2, P], F32, name="acc")
+            for m in range(2):
+                nc.tensor.transpose(f_t[:, m, :], f_sb[m][:, b * P : (b + 1) * P], ident[:])
+            own_t[b] = keep.tile([P, 2, P], F32, name="own_t%d" % b)
+            nc.scalar.activation(own_t[b][:], f_t[:], COPY, scale=shut_t[:, b : b + 1])
+        own = {}
+        for h in range(2):
+            for m in range(2):
+                own[m, h] = psum.tile([P, 2, P], F32, name="acc")
+                for e in range(2):
+                    nc.tensor.transpose(own[m, h][:, e, :], own_t[2 * h + e][:, m, :], ident[:])
+
+        got = {(m, h): keep.tile([P, HALF], F32, name="got%d%d" % (m, h)) for m in range(2) for h in range(2)}
+
+        def fetch(m, h):
+            cols = slice(h * HALF, (h + 1) * HALF)
+            nc.vector.tensor_tensor(got[m, h][:], f_sb[m][:].indirect(src_sb[:, h * LIST_COLS : (h + 1) * LIST_COLS]), thru_sb[:, cols], MULT)
+
+        def finish(m, h):
+            cols = slice(h * HALF, (h + 1) * HALF)
+            res = keep.tile([P, HALF], F32, name="res%d%d" % (m, h))
+            nc.vector.tensor_tensor(res[:], own[m, h][:].rearrange("p e c -> p (e c)"), got[m, h][:], ADD)
+            nc.sync.dma_start(out[m * P : (m + 1) * P, cols], res[:])
+
+        fetch(0, 0)
+        fetch(0, 1)
+        fetch(1, 0)
+        finish(0, 0)
+        finish(1, 0)
+        fetch(1, 1)
+        finish(0, 1)
+        finish(1, 1)

@@ -1,7 +1,6 @@
 from contextlib import ExitStack
 
 import concourse.mybir as mybir
-from concourse.masks import make_identity
 
 K, T, S, H, N = 512, 2048, 512, 512, 256
 FLOPS = 2 * K * H * S + 2 * H * N * S
@@ -33,87 +32,94 @@ def tile_picked_ylbm_part_p_kernel(tc, x_words, x_scales, w1, w2, eq, rate, thru
         src_sb = keep.tile([P, S // 16], U16, name="src_sb")
         xw = keep.tile([P, T], U32, name="xw", align_bytes=64)
         xs = keep.tile([P, T], U8, name="xs", align_bytes=64)
-        w1_raw = keep.tile([P, PACK, H], F32, name="w1_raw")
+        w1_raw = [keep.tile([P, PACK, HALF], F32, name="w1_raw%d" % h) for h in range(2)]
         w2_raw = keep.tile([P, PACK, N], F32, name="w2_raw")
-        eq_sb = [keep.tile([P, 2, S], F32, name="eq%d" % u) for u in range(2)]
+        eq_lo = keep.tile([P, PACK, HALF], F32, name="eq_lo")
+        eq_hi = [keep.tile([P, 2, HALF], F32, name="eq_hi%d" % e) for e in range(2)]
+        eq_pl = {(t, h): (eq_hi[t // 2][:, t % 2, :] if h else eq_lo[:, t, :]) for t in range(PACK) for h in range(2)}
         rate_sb = keep.tile([P, PACK], F32, name="rate_sb")
         keep_sb = keep.tile([P, PACK], F32, name="keep_sb")
         thru_sb = keep.tile([P, S], F32, name="thru_sb")
-        shut_t = keep.tile([P, S // P], F32, name="shut_t")
-        ident = keep.tile([P, P], F32, name="ident")
+        shut_sb = keep.tile([P, S], F32, name="shut_sb")
 
         nc.vector.memset(xs[:].bitcast(I32), 0)
-        nc.gpsimd.dma_start(rate_sb[:], rate.rearrange("(p t) o -> p (t o)", t=PACK))
-        make_identity(nc, ident[:])
-        nc.scalar.activation(keep_sb[:], rate_sb[:], COPY, scale=-1.0, bias=1.0)
 
         eq_rows = eq.rearrange("(p t) c -> p t c", t=PACK)
         w1_rows = w1.rearrange("(p j) c -> p j c", j=PACK)
-        nc.sync.dma_start(w1_raw[:, 0:2, :], w1_rows[:, 0:2, :])
+        nc.sync.dma_start(w1_raw[0][:], w1_rows[:, :, 0:HALF])
         nc.sync.dma_start(offs_sb[:], offs)
         for q in range(4):
             nc.sync.dma_start(xs[32 * q : 32 * q + 4, :].bitcast(I32), x_scales[0, 4 * q : 4 * q + 4, :].bitcast(I32))
-        nc.sync.dma_start(w1_raw[:, 2:4, :], w1_rows[:, 2:4, :])
         nc.sync.dma_start(xw[:].bitcast(I32), x_words[0].rearrange("p c r -> p (c r)").bitcast(I32))
+        nc.sync.dma_start(w1_raw[1][:], w1_rows[:, :, HALF : 2 * HALF])
+        nc.sync.dma_start(rate_sb[:], rate.rearrange("(p t) o -> p (t o)", t=PACK))
         nc.sync.dma_start(w2_raw[:], w2.rearrange("(p j) c -> p j c", j=PACK))
-        for u in range(2):
-            nc.sync.dma_start(eq_sb[u][:], eq_rows[:, 2 * u : 2 * u + 2, :])
+        nc.sync.dma_start(eq_lo[:], eq_rows[:, :, 0:HALF])
+        for e in range(2):
+            nc.sync.dma_start(eq_hi[e][:], eq_rows[:, 2 * e : 2 * e + 2, HALF:S])
+        nc.sync.dma_start(shut_sb[:], shut)
         nc.sync.dma_start(thru_sb[:], thru)
         nc.sync.dma_start(src_sb[:], src)
-        with nc.allow_non_contiguous_dma(reason="one value of shut to a partition"):
-            nc.sync.dma_start(shut_t[:], shut[0].rearrange("(b p) -> p b", p=P))
 
+        MH = P // 2
+        w1_bf = {(h, u): keep.tile([P, 2, MH, PACK], BF16, name="w1_bf%d%d" % (h, u), align_bytes=64) for h in range(2) for u in range(2)}
+        w1_codes = [keep.tile([P, P], U32, name="w1_codes%d" % t, align_bytes=64) for t in range(PACK)]
+        w1_sc = [keep.tile([P, P], U8, name="w1_sc%d" % t, align_bytes=64) for t in range(PACK)]
+
+        def w1_views(h, u):
+            return (w1_bf[h, u][:].rearrange("p t m j -> p m j t"),
+                    w1_raw[h][:].rearrange("p j (m t) -> p m j t", t=PACK)[:, :, :, 2 * u : 2 * u + 2])
+
+        def w1_quant(h, t):
+            nc.vector.quantize_mx(out=w1_codes[t][:, h * MH : (h + 1) * MH].bitcast(FP8X4), scales=w1_sc[t][:, h * MH : (h + 1) * MH],
+                                  in_=w1_bf[h, t // 2][:, t % 2, :, :].rearrange("p m j -> p (m j)"))
+
+        for u in range(2):
+            o, i = w1_views(0, u)
+            nc.scalar.activation(o, i, COPY)
         xs_g = keep.tile([P, S], U8, name="xs_g", align_bytes=64)
         nc.vector.tensor_copy(xs_g[:], xs[:].indirect(offs_sb[:]))
-
-        w1_bf = [keep.tile([P, 2, P, PACK], BF16, name="w1_bf%d" % u, align_bytes=64) for u in range(2)]
-        w1_codes = [keep.tile([P, 2, P], U32, name="w1_codes%d" % u, align_bytes=64) for u in range(2)]
-        w1_sc = [keep.tile([P, 2, P], U8, name="w1_sc%d" % u, align_bytes=64) for u in range(2)]
-
-        def w1_views(u):
-            return (w1_bf[u][:].rearrange("p t m j -> p m j t"),
-                    w1_raw[:].rearrange("p j (m t) -> p m j t", t=PACK)[:, :, :, 2 * u : 2 * u + 2])
-
-        o, i = w1_views(0)
+        for t in range(PACK):
+            w1_quant(0, t)
+        xw_g = keep.tile([P, S], U32, name="xw_g", align_bytes=64)
+        nc.vector.tensor_copy(xw_g[:], xw[:].indirect(offs_sb[:]))
+        o, i = w1_views(1, 0)
         nc.vector.tensor_copy(o, i)
-        o, i = w1_views(1)
+        o, i = w1_views(1, 1)
         nc.scalar.activation(o, i, COPY)
-        for u in range(2):
-            nc.vector.quantize_mx(out=w1_codes[u][:].rearrange("p t m -> p (t m)").bitcast(FP8X4), scales=w1_sc[u][:].rearrange("p t m -> p (t m)"),
-                                  in_=w1_bf[u][:].rearrange("p t m j -> p (t m j)"))
+        for t in range(PACK):
+            w1_quant(1, t)
 
-        xw_g = [keep.tile([P, HALF], U32, name="xw_g%d" % h, align_bytes=64) for h in range(2)]
-        for h in range(2):
-            nc.vector.tensor_copy(xw_g[h][:], xw[:].indirect(offs_sb[:, h * LIST_COLS : (h + 1) * LIST_COLS]))
-
+        nc.scalar.activation(keep_sb[:], rate_sb[:], COPY, scale=-1.0, bias=1.0)
         kept = {}
-        for u in range(2):
-            for h in range(2):
-                for e in range(2):
-                    t = 2 * u + e
+        order = [(t, h) for h in range(2) for t in range(PACK)]
+        for t, h in order:
+            for u in [t // 2]:
+                for e in [t % 2]:
                     y = psum.tile([P, HALF], F32, name="acc")
-                    nc.tensor.matmul_mx(out=y[:], lhsT=w1_codes[u][:, e, :].bitcast(FP8X4), lhsT_scale=w1_sc[u][:, e, :],
-                                        rhs=xw_g[h][:].bitcast(FP8X4), rhs_scale=xs_g[:, h * HALF : (h + 1) * HALF],
+                    nc.tensor.matmul_mx(out=y[:], lhsT=w1_codes[t][:].bitcast(FP8X4), lhsT_scale=w1_sc[t][:],
+                                        rhs=xw_g[:, h * HALF : (h + 1) * HALF].bitcast(FP8X4), rhs_scale=xs_g[:, h * HALF : (h + 1) * HALF],
                                         start=True, stop=True)
                     kept[h, t] = keep.tile([P, HALF], F32, name="kept%d%d" % (h, t))
                     nc.scalar.activation(kept[h, t][:], y[:], COPY, scale=keep_sb[:, t : t + 1])
 
-        w2_bf = keep.tile([P, N, PACK], BF16, name="w2_bf", align_bytes=64)
-        nc.vector.tensor_copy(w2_bf[:].rearrange("p (c i) j -> p c j i", i=4), w2_raw[:].rearrange("p j (c i) -> p c j i", i=4))
-        w2_codes = keep.tile([P, N], U32, name="w2_codes", align_bytes=64)
-        w2_sc = keep.tile([P, N], U8, name="w2_sc", align_bytes=64)
-        nc.vector.quantize_mx(out=w2_codes[:].bitcast(FP8X4), scales=w2_sc[:], in_=w2_bf[:].rearrange("p c j -> p (c j)"))
+        w2_bf = [keep.tile([P, P, PACK], BF16, name="w2_bf%d" % m, align_bytes=64) for m in range(2)]
+        w2_codes = [keep.tile([P, P], U32, name="w2_codes%d" % m, align_bytes=64) for m in range(2)]
+        w2_sc = [keep.tile([P, P], U8, name="w2_sc%d" % m, align_bytes=64) for m in range(2)]
+        for m in range(2):
+            nc.vector.tensor_copy(w2_bf[m][:].rearrange("p (c i) j -> p c j i", i=4), w2_raw[:, :, m * P : (m + 1) * P].rearrange("p j (c i) -> p c j i", i=4))
+        for m in range(2):
+            nc.vector.quantize_mx(out=w2_codes[m][:].bitcast(FP8X4), scales=w2_sc[m][:], in_=w2_bf[m][:].rearrange("p c j -> p (c j)"))
 
         rr_pl = [keep.tile([P, PACK, HALF], BF16, name="rr_pl%d" % h) for h in range(2)]
         rr_bf = [keep.tile([P, HALF, PACK], BF16, name="rr_bf%d" % h, align_bytes=64) for h in range(2)]
         rr_codes = keep.tile([P, S], U32, name="rr_codes", align_bytes=64)
         rr_sc = keep.tile([P, S], U8, name="rr_sc", align_bytes=64)
 
-        for u in range(2):
-            for h in range(2):
-                for e in range(2):
-                    t = 2 * u + e
-                    nc.vector.scalar_tensor_tensor(rr_pl[h][:, t, :], eq_sb[u][:, e, h * HALF : (h + 1) * HALF], rate_sb[:, t : t + 1], kept[h, t][:], MULT, ADD)
+        for t, h in order:
+            for u in [t // 2]:
+                for e in [t % 2]:
+                    nc.vector.scalar_tensor_tensor(rr_pl[h][:, t, :], eq_pl[t, h], rate_sb[:, t : t + 1], kept[h, t][:], MULT, ADD)
 
         def weave_views(h):
             return (rr_bf[h][:].rearrange("p (c i) t -> p c t i", i=4), rr_pl[h][:].rearrange("p t (c i) -> p c t i", i=4))
@@ -126,28 +132,19 @@ def tile_picked_ylbm_part_p_kernel(tc, x_words, x_scales, w1, w2, eq, rate, thru
             nc.vector.quantize_mx(out=rr_codes[:, h * HALF : (h + 1) * HALF].bitcast(FP8X4), scales=rr_sc[:, h * HALF : (h + 1) * HALF], in_=rr_bf[h][:].rearrange("p c t -> p (c t)"))
 
         f_sb = [keep.tile([P, S], F32, name="f_sb%d" % m) for m in range(2)]
-        for m, width in ((0, HALF), (1, S)):
+        for m, width in ((0, HALF), (1, HALF)):
             for c0 in range(0, S, width):
                 cols = slice(c0, c0 + width)
                 f = psum.tile([P, width], F32, name="acc")
-                nc.tensor.matmul_mx(out=f[:], lhsT=w2_codes[:, m * P : (m + 1) * P].bitcast(FP8X4),
-                                    lhsT_scale=w2_sc[:, m * P : (m + 1) * P],
+                nc.tensor.matmul_mx(out=f[:], lhsT=w2_codes[m][:].bitcast(FP8X4),
+                                    lhsT_scale=w2_sc[m][:],
                                     rhs=rr_codes[:, cols].bitcast(FP8X4), rhs_scale=rr_sc[:, cols], start=True, stop=True)
                 nc.scalar.copy(f_sb[m][:, cols], f[:])
 
-        own_t = {}
-        for b in range(S // P):
-            f_t = psum.tile([P, 2, P], F32, name="acc")
-            for m in range(2):
-                nc.tensor.transpose(f_t[:, m, :], f_sb[m][:, b * P : (b + 1) * P], ident[:])
-            own_t[b] = keep.tile([P, 2, P], F32, name="own_t%d" % b)
-            nc.scalar.activation(own_t[b][:], f_t[:], COPY, scale=shut_t[:, b : b + 1])
-        own = {}
-        for h in range(2):
-            for m in range(2):
-                own[m, h] = psum.tile([P, 2, P], F32, name="acc")
-                for e in range(2):
-                    nc.tensor.transpose(own[m, h][:, e, :], own_t[2 * h + e][:, m, :], ident[:])
+        own = [keep.tile([P, S], F32, name="own%d" % m) for m in range(2)]
+
+        def bounce(m, c0, c1):
+            nc.vector.tensor_tensor(own[m][:, c0:c1], f_sb[m][:, c0:c1], shut_sb[:, c0:c1], MULT)
 
         got = {(m, h): keep.tile([P, HALF], F32, name="got%d%d" % (m, h)) for m in range(2) for h in range(2)}
 
@@ -158,14 +155,18 @@ def tile_picked_ylbm_part_p_kernel(tc, x_words, x_scales, w1, w2, eq, rate, thru
         def finish(m, h):
             cols = slice(h * HALF, (h + 1) * HALF)
             res = keep.tile([P, HALF], F32, name="res%d%d" % (m, h))
-            nc.vector.tensor_tensor(res[:], own[m, h][:].rearrange("p e c -> p (e c)"), got[m, h][:], ADD)
+            nc.vector.tensor_tensor(res[:], own[m][:, cols], got[m, h][:], ADD)
             nc.sync.dma_start(out[m * P : (m + 1) * P, cols], res[:])
 
+        bounce(0, 0, HALF)
         fetch(0, 0)
         fetch(0, 1)
-        fetch(1, 0)
+        bounce(0, HALF, S)
         finish(0, 0)
-        finish(1, 0)
-        fetch(1, 1)
+        bounce(1, 0, HALF)
+        fetch(1, 0)
         finish(0, 1)
+        bounce(1, HALF, S)
+        fetch(1, 1)
+        finish(1, 0)
         finish(1, 1)

@@ -31,12 +31,11 @@ def tile_picked_ylbm_part_p_kernel(tc, x_words, x_scales, w1, w2, eq, rate, thru
         offs_sb = keep.tile([P, S // 16], U16, name="offs_sb")
         src_sb = keep.tile([P, S // 16], U16, name="src_sb")
         xw = keep.tile([P, T], U32, name="xw", align_bytes=64)
-        xs = keep.tile([P, T], U8, name="xs", align_bytes=64)
+        xs = keep.tile([P, T], U8, name="xs", tag="xs", align_bytes=64)
         w1_raw = [keep.tile([P, PACK, HALF], F32, name="w1_raw%d" % h) for h in range(2)]
         w2_raw = keep.tile([P, PACK, N], F32, name="w2_raw")
-        eq_lo = keep.tile([P, PACK, HALF], F32, name="eq_lo")
-        eq_hi = [keep.tile([P, 2, HALF], F32, name="eq_hi%d" % e) for e in range(2)]
-        eq_pl = {(t, h): (eq_hi[t // 2][:, t % 2, :] if h else eq_lo[:, t, :]) for t in range(PACK) for h in range(2)}
+        eq_sb = {(h, e): keep.tile([P, 2, HALF], F32, name="eq_sb%d%d" % (h, e)) for h in range(2) for e in range(2)}
+        eq_pl = {(t, h): eq_sb[h, t // 2][:, t % 2, :] for t in range(PACK) for h in range(2)}
         rate_sb = keep.tile([P, PACK], F32, name="rate_sb")
         keep_sb = keep.tile([P, PACK], F32, name="keep_sb")
         thru_sb = keep.tile([P, S], F32, name="thru_sb")
@@ -53,17 +52,16 @@ def tile_picked_ylbm_part_p_kernel(tc, x_words, x_scales, w1, w2, eq, rate, thru
         nc.sync.dma_start(xw[:].bitcast(I32), x_words[0].rearrange("p c r -> p (c r)").bitcast(I32))
         nc.sync.dma_start(w1_raw[1][:], w1_rows[:, :, HALF : 2 * HALF])
         nc.sync.dma_start(rate_sb[:], rate.rearrange("(p t) o -> p (t o)", t=PACK))
+        for h in range(2):
+            for e in range(2):
+                nc.sync.dma_start(eq_sb[h, e][:], eq_rows[:, 2 * e : 2 * e + 2, h * HALF : (h + 1) * HALF])
         nc.sync.dma_start(w2_raw[:], w2.rearrange("(p j) c -> p j c", j=PACK))
-        nc.sync.dma_start(eq_lo[:], eq_rows[:, :, 0:HALF])
-        for e in range(2):
-            nc.sync.dma_start(eq_hi[e][:], eq_rows[:, 2 * e : 2 * e + 2, HALF:S])
         nc.sync.dma_start(shut_sb[:], shut)
         nc.sync.dma_start(thru_sb[:], thru)
         nc.sync.dma_start(src_sb[:], src)
 
         MH = P // 2
         w1_bf = {(h, u): keep.tile([P, 2, MH, PACK], BF16, name="w1_bf%d%d" % (h, u), align_bytes=64) for h in range(2) for u in range(2)}
-        w1_codes = [keep.tile([P, P], U32, name="w1_codes%d" % t, align_bytes=64) for t in range(PACK)]
         w1_sc = [keep.tile([P, P], U8, name="w1_sc%d" % t, align_bytes=64) for t in range(PACK)]
 
         def w1_views(h, u):
@@ -79,6 +77,8 @@ def tile_picked_ylbm_part_p_kernel(tc, x_words, x_scales, w1, w2, eq, rate, thru
             nc.scalar.activation(o, i, COPY)
         xs_g = keep.tile([P, S], U8, name="xs_g", align_bytes=64)
         nc.vector.tensor_copy(xs_g[:], xs[:].indirect(offs_sb[:]))
+        w1_all = keep.tile([P, PACK, P], U32, name="w1_codes", tag="xs", align_bytes=64)
+        w1_codes = [w1_all[:, t, :] for t in range(PACK)]
         for t in range(PACK):
             w1_quant(0, t)
         xw_g = keep.tile([P, S], U32, name="xw_g", align_bytes=64)
@@ -91,45 +91,43 @@ def tile_picked_ylbm_part_p_kernel(tc, x_words, x_scales, w1, w2, eq, rate, thru
             w1_quant(1, t)
 
         nc.scalar.activation(keep_sb[:], rate_sb[:], COPY, scale=-1.0, bias=1.0)
-        kept = {}
-        order = [(t, h) for h in range(2) for t in range(PACK)]
-        for t, h in order:
-            for u in [t // 2]:
-                for e in [t % 2]:
-                    y = psum.tile([P, HALF], F32, name="acc")
-                    nc.tensor.matmul_mx(out=y[:], lhsT=w1_codes[t][:].bitcast(FP8X4), lhsT_scale=w1_sc[t][:],
-                                        rhs=xw_g[:, h * HALF : (h + 1) * HALF].bitcast(FP8X4), rhs_scale=xs_g[:, h * HALF : (h + 1) * HALF],
-                                        start=True, stop=True)
-                    kept[h, t] = keep.tile([P, HALF], F32, name="kept%d%d" % (h, t))
-                    nc.scalar.activation(kept[h, t][:], y[:], COPY, scale=keep_sb[:, t : t + 1])
-
-        w2_bf = [keep.tile([P, P, PACK], BF16, name="w2_bf%d" % m, align_bytes=64) for m in range(2)]
-        w2_codes = [keep.tile([P, P], U32, name="w2_codes%d" % m, align_bytes=64) for m in range(2)]
-        w2_sc = [keep.tile([P, P], U8, name="w2_sc%d" % m, align_bytes=64) for m in range(2)]
-        for m in range(2):
-            nc.vector.tensor_copy(w2_bf[m][:].rearrange("p (c i) j -> p c j i", i=4), w2_raw[:, :, m * P : (m + 1) * P].rearrange("p j (c i) -> p c j i", i=4))
-        for m in range(2):
-            nc.vector.quantize_mx(out=w2_codes[m][:].bitcast(FP8X4), scales=w2_sc[m][:], in_=w2_bf[m][:].rearrange("p c j -> p (c j)"))
-
         rr_pl = [keep.tile([P, PACK, HALF], BF16, name="rr_pl%d" % h) for h in range(2)]
         rr_bf = [keep.tile([P, HALF, PACK], BF16, name="rr_bf%d" % h, align_bytes=64) for h in range(2)]
         rr_codes = keep.tile([P, S], U32, name="rr_codes", align_bytes=64)
         rr_sc = keep.tile([P, S], U8, name="rr_sc", align_bytes=64)
+        for h in range(2):
+            for t in range(PACK):
+                pull = keep.tile([P, HALF], F32, name="pull%d%d" % (h, t))
+                nc.scalar.activation(pull[:], eq_pl[t, h], COPY, scale=rate_sb[:, t : t + 1])
+                y = psum.tile([P, HALF], F32, name="acc")
+                nc.tensor.matmul_mx(out=y[:], lhsT=w1_codes[t].bitcast(FP8X4), lhsT_scale=w1_sc[t][:],
+                                    rhs=xw_g[:, h * HALF : (h + 1) * HALF].bitcast(FP8X4), rhs_scale=xs_g[:, h * HALF : (h + 1) * HALF],
+                                    start=True, stop=True)
+                nc.vector.scalar_tensor_tensor(rr_pl[h][:, t, :], y[:], keep_sb[:, t : t + 1], pull[:], MULT, ADD)
 
-        for t, h in order:
-            for u in [t // 2]:
-                for e in [t % 2]:
-                    nc.vector.scalar_tensor_tensor(rr_pl[h][:, t, :], eq_pl[t, h], rate_sb[:, t : t + 1], kept[h, t][:], MULT, ADD)
+        w2_bf = [keep.tile([P, P, PACK], BF16, name="w2_bf%d" % m, align_bytes=64) for m in range(2)]
+        w2_codes = [keep.tile([P, P], U32, name="w2_codes%d" % m, align_bytes=64) for m in range(2)]
+        w2_sc = [keep.tile([P, P], U8, name="w2_sc%d" % m, align_bytes=64) for m in range(2)]
 
         def weave_views(h):
             return (rr_bf[h][:].rearrange("p (c i) t -> p c t i", i=4), rr_pl[h][:].rearrange("p t (c i) -> p c t i", i=4))
 
+        def rr_quant(h):
+            nc.vector.quantize_mx(out=rr_codes[:, h * HALF : (h + 1) * HALF].bitcast(FP8X4), scales=rr_sc[:, h * HALF : (h + 1) * HALF], in_=rr_bf[h][:].rearrange("p c t -> p (c t)"))
+
+        def w2_quant(m):
+            nc.vector.quantize_mx(out=w2_codes[m][:].bitcast(FP8X4), scales=w2_sc[m][:], in_=w2_bf[m][:].rearrange("p c j -> p (c j)"))
+
         o, i = weave_views(0)
         nc.scalar.copy(o, i)
+        for m in range(2):
+            nc.scalar.activation(w2_bf[m][:].rearrange("p (c i) j -> p c j i", i=4), w2_raw[:, :, m * P : (m + 1) * P].rearrange("p j (c i) -> p c j i", i=4), COPY)
         o, i = weave_views(1)
         nc.vector.tensor_copy(o, i)
-        for h in range(2):
-            nc.vector.quantize_mx(out=rr_codes[:, h * HALF : (h + 1) * HALF].bitcast(FP8X4), scales=rr_sc[:, h * HALF : (h + 1) * HALF], in_=rr_bf[h][:].rearrange("p c t -> p (c t)"))
+        rr_quant(0)
+        w2_quant(0)
+        rr_quant(1)
+        w2_quant(1)
 
         f_sb = [keep.tile([P, S], F32, name="f_sb%d" % m) for m in range(2)]
         for m, width in ((0, HALF), (1, HALF)):

@@ -32,7 +32,7 @@ def tile_picked_ylbm_part_p_kernel(tc, x_words, x_scales, w1, w2, eq, rate, thru
         src_sb = keep.tile([P, S // 16], U16, name="src_sb")
         xw = keep.tile([P, T], U32, name="xw", align_bytes=64)
         xs = keep.tile([P, T], U8, name="xs", tag="xs", align_bytes=64)
-        w1_raw = [keep.tile([P, PACK, HALF], F32, name="w1_raw%d" % h) for h in range(2)]
+        w1_raw = [keep.tile([P, 2, H], F32, name="w1_raw%d" % e) for e in range(2)]
         w2_raw = keep.tile([P, PACK, N], F32, name="w2_raw")
         eq_sb = {(h, e): keep.tile([P, 2, HALF], F32, name="eq_sb%d%d" % (h, e)) for h in range(2) for e in range(2)}
         eq_pl = {(t, h): eq_sb[h, t // 2][:, t % 2, :] for t in range(PACK) for h in range(2)}
@@ -45,12 +45,13 @@ def tile_picked_ylbm_part_p_kernel(tc, x_words, x_scales, w1, w2, eq, rate, thru
 
         eq_rows = eq.rearrange("(p t) c -> p t c", t=PACK)
         w1_rows = w1.rearrange("(p j) c -> p j c", j=PACK)
-        nc.sync.dma_start(w1_raw[0][:], w1_rows[:, :, 0:HALF])
+        nc.sync.dma_start(w1_raw[0][:], w1_rows[:, 0:2, :])
         nc.sync.dma_start(offs_sb[:], offs)
-        for q in range(4):
-            nc.sync.dma_start(xs[32 * q : 32 * q + 4, :].bitcast(I32), x_scales[0, 4 * q : 4 * q + 4, :].bitcast(I32))
+        scale_rows = x_scales[0].rearrange("(q r) c -> r q c", r=4)
+        for r in range(4):
+            nc.sync.dma_start(xs[r:P:32, :].bitcast(I32), scale_rows[r].bitcast(I32))
+        nc.sync.dma_start(w1_raw[1][:], w1_rows[:, 2:4, :])
         nc.sync.dma_start(xw[:].bitcast(I32), x_words[0].rearrange("p c r -> p (c r)").bitcast(I32))
-        nc.sync.dma_start(w1_raw[1][:], w1_rows[:, :, HALF : 2 * HALF])
         nc.sync.dma_start(rate_sb[:], rate.rearrange("(p t) o -> p (t o)", t=PACK))
         for h in range(2):
             for e in range(2):
@@ -60,78 +61,84 @@ def tile_picked_ylbm_part_p_kernel(tc, x_words, x_scales, w1, w2, eq, rate, thru
         nc.sync.dma_start(thru_sb[:], thru)
         nc.sync.dma_start(src_sb[:], src)
 
-        MH = P // 2
-        w1_bf = {(h, u): keep.tile([P, 2, MH, PACK], BF16, name="w1_bf%d%d" % (h, u), align_bytes=64) for h in range(2) for u in range(2)}
-        w1_sc = [keep.tile([P, P], U8, name="w1_sc%d" % t, align_bytes=64) for t in range(PACK)]
+        w1_bf = [keep.tile([P, 2, P, PACK], BF16, name="w1_bf%d" % u, align_bytes=64) for u in range(2)]
+        w1_sc = [keep.tile([P, 2 * P], U8, name="w1_sc%d" % u, align_bytes=64) for u in range(2)]
 
-        def w1_views(h, u):
-            return (w1_bf[h, u][:].rearrange("p t m j -> p m j t"),
-                    w1_raw[h][:].rearrange("p j (m t) -> p m j t", t=PACK)[:, :, :, 2 * u : 2 * u + 2])
+        def w1_views(u, e):
+            return (w1_bf[u][:, :, :, 2 * e : 2 * e + 2].rearrange("p t m j -> p m j t"),
+                    w1_raw[e][:].rearrange("p j (m t) -> p m j t", t=PACK)[:, :, :, 2 * u : 2 * u + 2])
 
-        def w1_quant(h, t):
-            nc.vector.quantize_mx(out=w1_codes[t][:, h * MH : (h + 1) * MH].bitcast(FP8X4), scales=w1_sc[t][:, h * MH : (h + 1) * MH],
-                                  in_=w1_bf[h, t // 2][:, t % 2, :, :].rearrange("p m j -> p (m j)"))
+        def w1_quant(u):
+            nc.vector.quantize_mx(out=w1_codes[:, 2 * u * P : 2 * (u + 1) * P].bitcast(FP8X4), scales=w1_sc[u][:], in_=w1_bf[u][:].rearrange("p t m j -> p (t m j)"))
 
-        for u in range(2):
-            o, i = w1_views(0, u)
-            nc.scalar.activation(o, i, COPY)
         xs_g = keep.tile([P, S], U8, name="xs_g", align_bytes=64)
+        xw_g = [keep.tile([P, HALF], U32, name="xw_g%d" % h, align_bytes=64) for h in range(2)]
+        for u in range(2):
+            o, i = w1_views(u, 0)
+            nc.scalar.activation(o, i, COPY)
         nc.vector.tensor_copy(xs_g[:], xs[:].indirect(offs_sb[:]))
-        w1_all = keep.tile([P, PACK, P], U32, name="w1_codes", tag="xs", align_bytes=64)
-        w1_codes = [w1_all[:, t, :] for t in range(PACK)]
-        for t in range(PACK):
-            w1_quant(0, t)
-        xw_g = keep.tile([P, S], U32, name="xw_g", align_bytes=64)
-        nc.vector.tensor_copy(xw_g[:], xw[:].indirect(offs_sb[:]))
-        o, i = w1_views(1, 0)
+        o, i = w1_views(0, 1)
         nc.vector.tensor_copy(o, i)
         o, i = w1_views(1, 1)
         nc.scalar.activation(o, i, COPY)
-        for t in range(PACK):
-            w1_quant(1, t)
-
+        w1_codes = keep.tile([P, H], U32, name="w1_codes", tag="xs", align_bytes=64)
+        w1_quant(0)
+        w1_quant(1)
         nc.scalar.activation(keep_sb[:], rate_sb[:], COPY, scale=-1.0, bias=1.0)
-        rr_pl = [keep.tile([P, PACK, HALF], BF16, name="rr_pl%d" % h) for h in range(2)]
+        for h in range(2):
+            nc.vector.tensor_copy(xw_g[h][:], xw[:].indirect(offs_sb[:, h * LIST_COLS : (h + 1) * LIST_COLS]))
+
+        rr_pl = [keep.tile([P, PACK, HALF], BF16, name="rr_pl%d" % h, tag="planes%d" % h, align_bytes=64) for h in range(2)]
         rr_bf = [keep.tile([P, HALF, PACK], BF16, name="rr_bf%d" % h, align_bytes=64) for h in range(2)]
         rr_codes = keep.tile([P, S], U32, name="rr_codes", align_bytes=64)
         rr_sc = keep.tile([P, S], U8, name="rr_sc", align_bytes=64)
         for h in range(2):
             for t in range(PACK):
-                pull = keep.tile([P, HALF], F32, name="pull%d%d" % (h, t))
-                nc.scalar.activation(pull[:], eq_pl[t, h], COPY, scale=rate_sb[:, t : t + 1])
+                pull = keep.tile([P, HALF], F32, name="pull%d%d" % (h, t), tag="pull%d%d" % (h, t), align_bytes=64)
+                if h == 1 and t >= 2:
+                    nc.gpsimd.tensor_scalar(pull[:], eq_pl[t, h], rate_sb[:, t : t + 1], 0.0, MULT, ADD)
+                else:
+                    nc.scalar.activation(pull[:], eq_pl[t, h], COPY, scale=rate_sb[:, t : t + 1])
                 y = psum.tile([P, HALF], F32, name="acc")
-                nc.tensor.matmul_mx(out=y[:], lhsT=w1_codes[t].bitcast(FP8X4), lhsT_scale=w1_sc[t][:],
-                                    rhs=xw_g[:, h * HALF : (h + 1) * HALF].bitcast(FP8X4), rhs_scale=xs_g[:, h * HALF : (h + 1) * HALF],
+                nc.tensor.matmul_mx(out=y[:], lhsT=w1_codes[:, t * P : (t + 1) * P].bitcast(FP8X4), lhsT_scale=w1_sc[t // 2][:, (t % 2) * P : (t % 2 + 1) * P],
+                                    rhs=xw_g[h][:].bitcast(FP8X4), rhs_scale=xs_g[:, h * HALF : (h + 1) * HALF],
                                     start=True, stop=True)
                 nc.vector.scalar_tensor_tensor(rr_pl[h][:, t, :], y[:], keep_sb[:, t : t + 1], pull[:], MULT, ADD)
 
-        w2_bf = [keep.tile([P, P, PACK], BF16, name="w2_bf%d" % m, align_bytes=64) for m in range(2)]
         w2_codes = [keep.tile([P, P], U32, name="w2_codes%d" % m, align_bytes=64) for m in range(2)]
         w2_sc = [keep.tile([P, P], U8, name="w2_sc%d" % m, align_bytes=64) for m in range(2)]
 
-        def weave_views(h):
-            return (rr_bf[h][:].rearrange("p (c i) t -> p c t i", i=4), rr_pl[h][:].rearrange("p t (c i) -> p c t i", i=4))
+        def weave_views(c0, c1):
+            h, lo, hi = c0 // HALF, c0 % HALF, c0 % HALF + c1 - c0
+            return (rr_bf[h][:, lo:hi, :].rearrange("p (c i) t -> p c t i", i=4), rr_pl[h][:, :, lo:hi].rearrange("p t (c i) -> p c t i", i=4))
 
-        def rr_quant(h):
-            nc.vector.quantize_mx(out=rr_codes[:, h * HALF : (h + 1) * HALF].bitcast(FP8X4), scales=rr_sc[:, h * HALF : (h + 1) * HALF], in_=rr_bf[h][:].rearrange("p c t -> p (c t)"))
+        def rr_quant(c0, c1):
+            h, lo, hi = c0 // HALF, c0 % HALF, c0 % HALF + c1 - c0
+            nc.vector.quantize_mx(out=rr_codes[:, c0:c1].bitcast(FP8X4), scales=rr_sc[:, c0:c1], in_=rr_bf[h][:, lo:hi, :].rearrange("p c t -> p (c t)"))
 
         def w2_quant(m):
             nc.vector.quantize_mx(out=w2_codes[m][:].bitcast(FP8X4), scales=w2_sc[m][:], in_=w2_bf[m][:].rearrange("p c j -> p (c j)"))
 
-        o, i = weave_views(0)
+        w2_bf = [keep.tile([P, P, PACK], BF16, name="w2_bf%d" % m, tag="pull1%d" % (1 + 2 * m), align_bytes=64) for m in range(2)]
+
+        def w2_views(m):
+            return (w2_bf[m][:].rearrange("p (c i) j -> p c j i", i=4), w2_raw[:, :, m * P : (m + 1) * P].rearrange("p j (c i) -> p c j i", i=4))
+
+        o, i = weave_views(0, HALF)
         nc.scalar.copy(o, i)
         for m in range(2):
-            nc.scalar.activation(w2_bf[m][:].rearrange("p (c i) j -> p c j i", i=4), w2_raw[:, :, m * P : (m + 1) * P].rearrange("p j (c i) -> p c j i", i=4), COPY)
-        o, i = weave_views(1)
+            o, i = w2_views(m)
+            nc.scalar.activation(o, i, COPY)
+        o, i = weave_views(HALF, S)
         nc.vector.tensor_copy(o, i)
-        rr_quant(0)
+        rr_quant(0, HALF)
         w2_quant(0)
-        rr_quant(1)
+        rr_quant(HALF, S)
         w2_quant(1)
 
         f_sb = [keep.tile([P, S], F32, name="f_sb%d" % m) for m in range(2)]
         for m, width in ((0, HALF), (1, HALF)):
-            for c0 in range(0, S, width):
+            for c0 in (0, HALF):
                 cols = slice(c0, c0 + width)
                 f = psum.tile([P, width], F32, name="acc")
                 nc.tensor.matmul_mx(out=f[:], lhsT=w2_codes[m][:].bitcast(FP8X4),

@@ -1,6 +1,7 @@
 from contextlib import ExitStack
 
 import concourse.mybir as mybir
+from concourse.masks import make_identity
 
 K, T, S, H, N = 512, 2048, 512, 512, 256
 FLOPS = 2 * K * H * S + 2 * H * N * S
@@ -26,7 +27,8 @@ def tile_picked_ylbm_part_p_kernel(tc, x_words, x_scales, w1, w2, eq, rate, thru
     nc = tc.nc
     with ExitStack() as ctx:
         keep = ctx.enter_context(tc.tile_pool(name="keep", bufs=1))
-        psum = ctx.enter_context(tc.psum_pool(name="psum", bufs=8))
+        psum = ctx.enter_context(tc.psum_pool(name="psum", bufs=6))
+        psum_own = ctx.enter_context(tc.psum_pool(name="psum_own", bufs=1))
 
         offs_sb = keep.tile([P, S // 16], U16, name="offs_sb")
         src_sb = keep.tile([P, S // 16], U16, name="src_sb")
@@ -39,7 +41,10 @@ def tile_picked_ylbm_part_p_kernel(tc, x_words, x_scales, w1, w2, eq, rate, thru
         rate_sb = keep.tile([P, PACK], F32, name="rate_sb")
         keep_sb = keep.tile([P, PACK], F32, name="keep_sb")
         thru_sb = keep.tile([P, S], F32, name="thru_sb")
-        shut_sb = keep.tile([P, S], F32, name="shut_sb")
+        shut_sb = keep.tile([P, HALF], F32, name="shut_sb")
+        shut_col = keep.tile([P, PACK], F32, name="shut_col")
+        ident = keep.tile([P, P], F32, name="ident")
+        make_identity(nc, ident[:])
 
         nc.vector.memset(xs[:].bitcast(I32), 0)
 
@@ -57,9 +62,11 @@ def tile_picked_ylbm_part_p_kernel(tc, x_words, x_scales, w1, w2, eq, rate, thru
             for e in range(2):
                 nc.sync.dma_start(eq_sb[h, e][:], eq_rows[:, 2 * e : 2 * e + 2, h * HALF : (h + 1) * HALF])
         nc.sync.dma_start(w2_raw[:], w2.rearrange("(p j) c -> p j c", j=PACK))
-        nc.sync.dma_start(shut_sb[:], shut)
-        nc.sync.dma_start(thru_sb[:], thru)
         nc.sync.dma_start(src_sb[:], src)
+        nc.sync.dma_start(shut_sb[:], shut[:, 0:HALF])
+        nc.sync.dma_start(thru_sb[:], thru)
+        with nc.allow_non_contiguous_dma(reason="one value of shut to a partition"):
+            nc.sync.dma_start(shut_col[:], shut[0, :].rearrange("(b p) -> p b", p=P))
 
         w1_bf = [keep.tile([P, 2, P, PACK], BF16, name="w1_bf%d" % u, align_bytes=64) for u in range(2)]
         w1_sc = [keep.tile([P, 2 * P], U8, name="w1_sc%d" % u, align_bytes=64) for u in range(2)]
@@ -105,8 +112,10 @@ def tile_picked_ylbm_part_p_kernel(tc, x_words, x_scales, w1, w2, eq, rate, thru
                                     start=True, stop=True)
                 nc.vector.scalar_tensor_tensor(rr_pl[h][:, t, :], y[:], keep_sb[:, t : t + 1], pull[:], MULT, ADD)
 
-        w2_codes = [keep.tile([P, P], U32, name="w2_codes%d" % m, align_bytes=64) for m in range(2)]
-        w2_sc = [keep.tile([P, P], U8, name="w2_sc%d" % m, align_bytes=64) for m in range(2)]
+        w2_codes_all = keep.tile([P, N], U32, name="w2_codes", align_bytes=64)
+        w2_sc_all = keep.tile([P, N], U8, name="w2_sc", align_bytes=64)
+        w2_codes = [w2_codes_all[:, m * P : (m + 1) * P] for m in range(2)]
+        w2_sc = [w2_sc_all[:, m * P : (m + 1) * P] for m in range(2)]
 
         def weave_views(c0, c1):
             h, lo, hi = c0 // HALF, c0 % HALF, c0 % HALF + c1 - c0
@@ -117,7 +126,7 @@ def tile_picked_ylbm_part_p_kernel(tc, x_words, x_scales, w1, w2, eq, rate, thru
             nc.vector.quantize_mx(out=rr_codes[:, c0:c1].bitcast(FP8X4), scales=rr_sc[:, c0:c1], in_=rr_bf[h][:, lo:hi, :].rearrange("p c t -> p (c t)"))
 
         def w2_quant(m):
-            nc.vector.quantize_mx(out=w2_codes[m][:].bitcast(FP8X4), scales=w2_sc[m][:], in_=w2_bf[m][:].rearrange("p c j -> p (c j)"))
+            nc.vector.quantize_mx(out=w2_codes[m].bitcast(FP8X4), scales=w2_sc[m], in_=w2_bf[m][:].rearrange("p c j -> p (c j)"))
 
         w2_bf = [keep.tile([P, P, PACK], BF16, name="w2_bf%d" % m, tag="pull1%d" % (1 + 2 * m), align_bytes=64) for m in range(2)]
 
@@ -141,15 +150,26 @@ def tile_picked_ylbm_part_p_kernel(tc, x_words, x_scales, w1, w2, eq, rate, thru
             for c0 in (0, HALF):
                 cols = slice(c0, c0 + width)
                 f = psum.tile([P, width], F32, name="acc")
-                nc.tensor.matmul_mx(out=f[:], lhsT=w2_codes[m][:].bitcast(FP8X4),
-                                    lhsT_scale=w2_sc[m][:],
+                nc.tensor.matmul_mx(out=f[:], lhsT=w2_codes[m].bitcast(FP8X4),
+                                    lhsT_scale=w2_sc[m],
                                     rhs=rr_codes[:, cols].bitcast(FP8X4), rhs_scale=rr_sc[:, cols], start=True, stop=True)
                 nc.scalar.copy(f_sb[m][:, cols], f[:])
 
-        own = [keep.tile([P, S], F32, name="own%d" % m) for m in range(2)]
+        own_ps = [psum_own.tile([P, S], F32, name="own_ps%d" % m) for m in range(2)]
+        turned = [keep.tile([P, N], F32, name="turned%d" % b) for b in range(PACK)]
+        for b in (2, 3, 0, 1):
+            cells = slice(b * P, (b + 1) * P)
+            rows = slice(0 if b >= 2 else P, N)
+            f_turned = psum.tile([P, N], F32, name="acc")
+            nc.tensor.matmul_mx(out=f_turned[:, rows], lhsT=rr_codes[:, cells].bitcast(FP8X4), lhsT_scale=rr_sc[:, cells],
+                                rhs=w2_codes_all[:, rows].bitcast(FP8X4), rhs_scale=w2_sc_all[:, rows], start=True, stop=True)
+            nc.scalar.activation(turned[b][:, rows], f_turned[:, rows], COPY, scale=shut_col[:, b : b + 1])
+        for m, b in [(0, 2), (0, 3), (1, 2), (1, 3), (1, 0), (1, 1)]:
+            nc.tensor.transpose(own_ps[m][:, b * P : (b + 1) * P], turned[b][:, m * P : (m + 1) * P], ident[:])
 
-        def bounce(m, c0, c1):
-            nc.vector.tensor_tensor(own[m][:, c0:c1], f_sb[m][:, c0:c1], shut_sb[:, c0:c1], MULT)
+        own_sb = keep.tile([P, HALF], F32, name="own_sb")
+        own = {(m, h): own_ps[m][:, h * HALF : (h + 1) * HALF] for m in range(2) for h in range(2)}
+        own[0, 0] = own_sb[:]
 
         got = {(m, h): keep.tile([P, HALF], F32, name="got%d%d" % (m, h)) for m in range(2) for h in range(2)}
 
@@ -160,18 +180,15 @@ def tile_picked_ylbm_part_p_kernel(tc, x_words, x_scales, w1, w2, eq, rate, thru
         def finish(m, h):
             cols = slice(h * HALF, (h + 1) * HALF)
             res = keep.tile([P, HALF], F32, name="res%d%d" % (m, h))
-            nc.vector.tensor_tensor(res[:], own[m][:, cols], got[m, h][:], ADD)
+            nc.vector.tensor_tensor(res[:], got[m, h][:], own[m, h], ADD)
             nc.sync.dma_start(out[m * P : (m + 1) * P, cols], res[:])
 
-        bounce(0, 0, HALF)
+        nc.vector.tensor_tensor(own_sb[:], f_sb[0][:, 0:HALF], shut_sb[:], MULT)
         fetch(0, 0)
         fetch(0, 1)
-        bounce(0, HALF, S)
         finish(0, 0)
-        bounce(1, 0, HALF)
         fetch(1, 0)
-        finish(0, 1)
-        bounce(1, HALF, S)
         fetch(1, 1)
+        finish(0, 1)
         finish(1, 0)
         finish(1, 1)

@@ -44,9 +44,10 @@ def tile_picked_ylbm_part_p_kernel(tc, x_words, x_scales, w1, w2, eq, rate, thru
         shut_sb = keep.tile([P, HALF], F32, name="shut_sb")
         shut_col = keep.tile([P, PACK], F32, name="shut_col")
         ident = keep.tile([P, P], F32, name="ident")
-        make_identity(nc, ident[:])
 
         nc.vector.memset(xs[:].bitcast(I32), 0)
+        nc.vector.memset(ident[:], 0.0)
+        make_identity(nc, ident[:], nomemset=True)
 
         eq_rows = eq.rearrange("(p t) c -> p t c", t=PACK)
         w1_rows = w1.rearrange("(p j) c -> p j c", j=PACK)
@@ -133,21 +134,26 @@ def tile_picked_ylbm_part_p_kernel(tc, x_words, x_scales, w1, w2, eq, rate, thru
         def w2_views(m):
             return (w2_bf[m][:].rearrange("p (c i) j -> p c j i", i=4), w2_raw[:, :, m * P : (m + 1) * P].rearrange("p j (c i) -> p c j i", i=4))
 
-        o, i = weave_views(0, HALF)
+        o, i = weave_views(0, P)
         nc.scalar.copy(o, i)
-        for m in range(2):
-            o, i = w2_views(m)
-            nc.scalar.activation(o, i, COPY)
+        o, i = weave_views(P, HALF)
+        nc.scalar.copy(o, i)
+        o, i = w2_views(0)
+        nc.scalar.activation(o, i, COPY)
+        o, i = w2_views(1)
+        nc.scalar.activation(o, i, COPY)
+        rr_quant(0, P)
         o, i = weave_views(HALF, S)
         nc.vector.tensor_copy(o, i)
-        rr_quant(0, HALF)
+        rr_quant(P, HALF)
         w2_quant(0)
-        rr_quant(HALF, S)
+        for c0 in range(HALF, S, P):
+            rr_quant(c0, c0 + P)
         w2_quant(1)
 
         f_sb = [keep.tile([P, S], F32, name="f_sb%d" % m) for m in range(2)]
-        for m, width in ((0, HALF), (1, HALF)):
-            for c0 in (0, HALF):
+        for m, width in ((0, P), (1, HALF)):
+            for c0 in range(0, S, width):
                 cols = slice(c0, c0 + width)
                 f = psum.tile([P, width], F32, name="acc")
                 nc.tensor.matmul_mx(out=f[:], lhsT=w2_codes[m].bitcast(FP8X4),

@@ -35,7 +35,7 @@ def tile_picked_ylbm_part_p_kernel(tc, x_words, x_scales, w1, w2, eq, rate, thru
         xw = keep.tile([P, T], U32, name="xw", align_bytes=64)
         xs = keep.tile([P, T], U8, name="xs", tag="xs", align_bytes=64)
         w1_raw = [keep.tile([P, 2, H], F32, name="w1_raw%d" % e) for e in range(2)]
-        w2_raw = keep.tile([P, PACK, N], F32, name="w2_raw")
+        w2_raw = [keep.tile([P, PACK, P], F32, name="w2_raw%d" % m) for m in range(2)]
         eq_sb = {(h, e): keep.tile([P, 2, HALF], F32, name="eq_sb%d%d" % (h, e)) for h in range(2) for e in range(2)}
         eq_pl = {(t, h): eq_sb[h, t // 2][:, t % 2, :] for t in range(PACK) for h in range(2)}
         rate_sb = keep.tile([P, PACK], F32, name="rate_sb")
@@ -62,7 +62,9 @@ def tile_picked_ylbm_part_p_kernel(tc, x_words, x_scales, w1, w2, eq, rate, thru
         for h in range(2):
             for e in range(2):
                 nc.sync.dma_start(eq_sb[h, e][:], eq_rows[:, 2 * e : 2 * e + 2, h * HALF : (h + 1) * HALF])
-        nc.sync.dma_start(w2_raw[:], w2.rearrange("(p j) c -> p j c", j=PACK))
+        w2_rows = w2.rearrange("(p j) c -> p j c", j=PACK)
+        for m in range(2):
+            nc.sync.dma_start(w2_raw[m][:], w2_rows[:, :, m * P : (m + 1) * P])
         nc.sync.dma_start(src_sb[:], src)
         nc.sync.dma_start(shut_sb[:], shut[:, 0:HALF])
         nc.sync.dma_start(thru_sb[:], thru)
@@ -101,6 +103,7 @@ def tile_picked_ylbm_part_p_kernel(tc, x_words, x_scales, w1, w2, eq, rate, thru
         rr_codes = keep.tile([P, S], U32, name="rr_codes", align_bytes=64)
         rr_sc = keep.tile([P, S], U8, name="rr_sc", align_bytes=64)
         for h in range(2):
+            late = []
             for t in range(PACK):
                 pull = keep.tile([P, HALF], F32, name="pull%d%d" % (h, t), tag="pull%d%d" % (h, t), align_bytes=64)
                 if h == 1 and t >= 2:
@@ -111,7 +114,13 @@ def tile_picked_ylbm_part_p_kernel(tc, x_words, x_scales, w1, w2, eq, rate, thru
                 nc.tensor.matmul_mx(out=y[:], lhsT=w1_codes[:, t * P : (t + 1) * P].bitcast(FP8X4), lhsT_scale=w1_sc[t // 2][:, (t % 2) * P : (t % 2 + 1) * P],
                                     rhs=xw_g[h][:].bitcast(FP8X4), rhs_scale=xs_g[:, h * HALF : (h + 1) * HALF],
                                     start=True, stop=True)
-                nc.vector.scalar_tensor_tensor(rr_pl[h][:, t, :], y[:], keep_sb[:, t : t + 1], pull[:], MULT, ADD)
+                if h == 1 or t < 2:
+                    nc.vector.scalar_tensor_tensor(rr_pl[h][:, t, :], y[:], keep_sb[:, t : t + 1], pull[:], MULT, ADD)
+                else:
+                    late.append((t, y, pull))
+            for c0 in range(0, HALF, P):
+                for t, y, pull in late:
+                    nc.vector.scalar_tensor_tensor(rr_pl[h][:, t, c0 : c0 + P], y[:, c0 : c0 + P], keep_sb[:, t : t + 1], pull[:, c0 : c0 + P], MULT, ADD)
 
         w2_codes_all = keep.tile([P, N], U32, name="w2_codes", align_bytes=64)
         w2_sc_all = keep.tile([P, N], U8, name="w2_sc", align_bytes=64)
@@ -132,7 +141,7 @@ def tile_picked_ylbm_part_p_kernel(tc, x_words, x_scales, w1, w2, eq, rate, thru
         w2_bf = [keep.tile([P, P, PACK], BF16, name="w2_bf%d" % m, tag="pull1%d" % (1 + 2 * m), align_bytes=64) for m in range(2)]
 
         def w2_views(m):
-            return (w2_bf[m][:].rearrange("p (c i) j -> p c j i", i=4), w2_raw[:, :, m * P : (m + 1) * P].rearrange("p j (c i) -> p c j i", i=4))
+            return (w2_bf[m][:].rearrange("p (c i) j -> p c j i", i=4), w2_raw[m][:].rearrange("p j (c i) -> p c j i", i=4))
 
         o, i = weave_views(0, P)
         nc.scalar.copy(o, i)

@@ -21,35 +21,33 @@ P = 128
 PACK = 4
 HALF = S // 2
 LIST_COLS = HALF // 16
+W2_SHARE = 64
+KIB = 1024
 
 
 def tile_picked_ylbm_part_p_kernel(tc, x_words, x_scales, w1, w2, eq, rate, thru, shut, offs, src, out):
     nc = tc.nc
     with ExitStack() as ctx:
         keep = ctx.enter_context(tc.tile_pool(name="keep", bufs=1))
+        head = ctx.enter_context(tc.tile_pool(name="head", bufs=1))
+        mid = ctx.enter_context(tc.tile_pool(name="mid", bufs=1))
         psum = ctx.enter_context(tc.psum_pool(name="psum", bufs=6))
         psum_own = ctx.enter_context(tc.psum_pool(name="psum_own", bufs=1))
 
         offs_sb = keep.tile([P, S // 16], U16, name="offs_sb")
         src_sb = keep.tile([P, S // 16], U16, name="src_sb")
         xw = keep.tile([P, T], U32, name="xw", align_bytes=64)
-        xs = keep.tile([P, T], U8, name="xs", tag="xs", align_bytes=64)
+        xs = head.tile([P, T], U8, name="xs", align_bytes=64, offset=KIB)
+        xs_g = keep.tile([P, S], U8, name="xs_g", align_bytes=64)
         w1_raw = [keep.tile([P, 2, H], F32, name="w1_raw%d" % e) for e in range(2)]
-        w2_raw = [keep.tile([P, PACK, P], F32, name="w2_raw%d" % m) for m in range(2)]
-        eq_sb = {(h, e): keep.tile([P, 2, HALF], F32, name="eq_sb%d%d" % (h, e)) for h in range(2) for e in range(2)}
-        eq_pl = {(t, h): eq_sb[h, t // 2][:, t % 2, :] for t in range(PACK) for h in range(2)}
         rate_sb = keep.tile([P, PACK], F32, name="rate_sb")
         keep_sb = keep.tile([P, PACK], F32, name="keep_sb")
-        thru_sb = keep.tile([P, S], F32, name="thru_sb")
-        shut_sb = keep.tile([P, HALF], F32, name="shut_sb")
-        shut_col = keep.tile([P, PACK], F32, name="shut_col")
         ident = keep.tile([P, P], F32, name="ident")
 
         nc.vector.memset(xs[:].bitcast(I32), 0)
         nc.vector.memset(ident[:], 0.0)
         make_identity(nc, ident[:], nomemset=True)
 
-        eq_rows = eq.rearrange("(p t) c -> p t c", t=PACK)
         w1_rows = w1.rearrange("(p j) c -> p j c", j=PACK)
         nc.sync.dma_start(w1_raw[0][:], w1_rows[:, 0:2, :])
         nc.sync.dma_start(offs_sb[:], offs)
@@ -59,54 +57,60 @@ def tile_picked_ylbm_part_p_kernel(tc, x_words, x_scales, w1, w2, eq, rate, thru
         nc.sync.dma_start(w1_raw[1][:], w1_rows[:, 2:4, :])
         nc.sync.dma_start(xw[:].bitcast(I32), x_words[0].rearrange("p c r -> p (c r)").bitcast(I32))
         nc.sync.dma_start(rate_sb[:], rate.rearrange("(p t) o -> p (t o)", t=PACK))
+
+        late = keep.tile([P, 8 * S], F32, name="late", align_bytes=64)
+        eq_sb = {(h, e): late[:, (2 * h + e) * S : (2 * h + e + 1) * S].rearrange("p (t c) -> p t c", t=2) for h in range(2) for e in range(2)}
+        eq_pl = {(t, h): late[:, (4 * h + t) * HALF : (4 * h + t + 1) * HALF] for t in range(PACK) for h in range(2)}
+        w2_raw = [late[:, (4 + m) * S : (5 + m) * S].rearrange("p (j c) -> p j c", j=PACK) for m in range(2)]
+        thru_sb = late[:, 6 * S : 7 * S]
+        shut_sb = late[:, 7 * S : 7 * S + HALF]
+        shut_col = late[:, 7 * S + HALF : 7 * S + HALF + PACK]
+        eq_rows = eq.rearrange("(p t) c -> p t c", t=PACK)
         for h in range(2):
             for e in range(2):
-                nc.sync.dma_start(eq_sb[h, e][:], eq_rows[:, 2 * e : 2 * e + 2, h * HALF : (h + 1) * HALF])
+                nc.sync.dma_start(eq_sb[h, e], eq_rows[:, 2 * e : 2 * e + 2, h * HALF : (h + 1) * HALF])
         w2_rows = w2.rearrange("(p j) c -> p j c", j=PACK)
         for m in range(2):
-            nc.sync.dma_start(w2_raw[m][:], w2_rows[:, :, m * P : (m + 1) * P])
+            nc.sync.dma_start(w2_raw[m], w2_rows[:, :, m * P : (m + 1) * P])
         nc.sync.dma_start(src_sb[:], src)
-        nc.sync.dma_start(shut_sb[:], shut[:, 0:HALF])
-        nc.sync.dma_start(thru_sb[:], thru)
+        nc.sync.dma_start(shut_sb, shut[:, 0:HALF])
+        nc.sync.dma_start(thru_sb, thru)
         with nc.allow_non_contiguous_dma(reason="one value of shut to a partition"):
-            nc.sync.dma_start(shut_col[:], shut[0, :].rearrange("(b p) -> p b", p=P))
+            nc.sync.dma_start(shut_col, shut[0, :].rearrange("(b p) -> p b", p=P))
 
         w1_bf = [keep.tile([P, 2, P, PACK], BF16, name="w1_bf%d" % u, align_bytes=64) for u in range(2)]
         w1_sc = [keep.tile([P, 2 * P], U8, name="w1_sc%d" % u, align_bytes=64) for u in range(2)]
+        w1_codes = head.tile([P, H], U32, name="w1_codes", align_bytes=64, offset=0)
 
         def w1_views(u, e):
             return (w1_bf[u][:, :, :, 2 * e : 2 * e + 2].rearrange("p t m j -> p m j t"),
                     w1_raw[e][:].rearrange("p j (m t) -> p m j t", t=PACK)[:, :, :, 2 * u : 2 * u + 2])
 
-        def w1_quant(u):
-            nc.vector.quantize_mx(out=w1_codes[:, 2 * u * P : 2 * (u + 1) * P].bitcast(FP8X4), scales=w1_sc[u][:], in_=w1_bf[u][:].rearrange("p t m j -> p (t m j)"))
-
-        xs_g = keep.tile([P, S], U8, name="xs_g", align_bytes=64)
-        xw_g = [keep.tile([P, HALF], U32, name="xw_g%d" % h, align_bytes=64) for h in range(2)]
         for u in range(2):
-            o, i = w1_views(u, 0)
-            nc.scalar.activation(o, i, COPY)
+            nc.scalar.activation(*w1_views(u, 0), COPY)
         nc.vector.tensor_copy(xs_g[:], xs[:].indirect(offs_sb[:]))
-        o, i = w1_views(0, 1)
-        nc.vector.tensor_copy(o, i)
-        o, i = w1_views(1, 1)
-        nc.scalar.activation(o, i, COPY)
-        w1_codes = keep.tile([P, H], U32, name="w1_codes", tag="xs", align_bytes=64)
-        w1_quant(0)
-        w1_quant(1)
+        nc.vector.tensor_copy(*w1_views(0, 1))
+        nc.scalar.activation(*w1_views(1, 1), COPY)
+        for u in range(2):
+            nc.vector.quantize_mx(out=w1_codes[:, 2 * u * P : 2 * (u + 1) * P].bitcast(FP8X4), scales=w1_sc[u][:], in_=w1_bf[u][:].rearrange("p t m j -> p (t m j)"))
         nc.scalar.activation(keep_sb[:], rate_sb[:], COPY, scale=-1.0, bias=1.0)
+        xw_g = [keep.tile([P, HALF], U32, name="xw_g%d" % h, align_bytes=64) for h in range(2)]
         for h in range(2):
             nc.vector.tensor_copy(xw_g[h][:], xw[:].indirect(offs_sb[:, h * LIST_COLS : (h + 1) * LIST_COLS]))
 
-        rr_pl = [keep.tile([P, PACK, HALF], BF16, name="rr_pl%d" % h, tag="planes%d" % h, align_bytes=64) for h in range(2)]
-        rr_bf = [keep.tile([P, HALF, PACK], BF16, name="rr_bf%d" % h, align_bytes=64) for h in range(2)]
-        rr_codes = keep.tile([P, S], U32, name="rr_codes", align_bytes=64)
-        rr_sc = keep.tile([P, S], U8, name="rr_sc", align_bytes=64)
+        rr_pl = [keep.tile([P, PACK, HALF], BF16, name="rr_pl%d" % h, align_bytes=64) for h in range(2)]
+        rr_bf = [keep.tile([P, HALF, PACK], BF16, name="rr_bf0", align_bytes=64)]
+        shared_bf = keep.tile([P, W2_SHARE + P, PACK], BF16, name="shared_bf", align_bytes=64)
+        rr_bf3 = keep.tile([P, P, PACK], BF16, name="rr_bf3", align_bytes=64)
+        woven = {(0, 0, P): rr_bf[0][:, 0:P, :], (0, P, HALF): rr_bf[0][:, P:HALF, :], (0, 0, HALF): rr_bf[0][:], (1, 0, P): shared_bf[:, W2_SHARE : W2_SHARE + P, :], (1, P, HALF): rr_bf3[:]}
         for h in range(2):
-            late = []
+            by_quarters = []
             for t in range(PACK):
-                pull = keep.tile([P, HALF], F32, name="pull%d%d" % (h, t), tag="pull%d%d" % (h, t), align_bytes=64)
-                if h == 1 and t >= 2:
+                if (h, t) == (1, 2):
+                    pull = mid.tile([P, HALF], F32, name="pull12", align_bytes=64, offset=KIB // 2)
+                else:
+                    pull = keep.tile([P, HALF], F32, name="pull%d%d" % (h, t), tag="pull%d%d" % (h, t), align_bytes=64)
+                if h == 1 and t < 2:
                     nc.gpsimd.tensor_scalar(pull[:], eq_pl[t, h], rate_sb[:, t : t + 1], 0.0, MULT, ADD)
                 else:
                     nc.scalar.activation(pull[:], eq_pl[t, h], COPY, scale=rate_sb[:, t : t + 1])
@@ -114,91 +118,81 @@ def tile_picked_ylbm_part_p_kernel(tc, x_words, x_scales, w1, w2, eq, rate, thru
                 nc.tensor.matmul_mx(out=y[:], lhsT=w1_codes[:, t * P : (t + 1) * P].bitcast(FP8X4), lhsT_scale=w1_sc[t // 2][:, (t % 2) * P : (t % 2 + 1) * P],
                                     rhs=xw_g[h][:].bitcast(FP8X4), rhs_scale=xs_g[:, h * HALF : (h + 1) * HALF],
                                     start=True, stop=True)
-                if h == 1 or t < 2:
+                if t < 2:
                     nc.vector.scalar_tensor_tensor(rr_pl[h][:, t, :], y[:], keep_sb[:, t : t + 1], pull[:], MULT, ADD)
                 else:
-                    late.append((t, y, pull))
+                    by_quarters.append((t, y, pull))
             for c0 in range(0, HALF, P):
-                for t, y, pull in late:
+                for t, y, pull in by_quarters:
                     nc.vector.scalar_tensor_tensor(rr_pl[h][:, t, c0 : c0 + P], y[:, c0 : c0 + P], keep_sb[:, t : t + 1], pull[:, c0 : c0 + P], MULT, ADD)
 
-        w2_codes_all = keep.tile([P, N], U32, name="w2_codes", align_bytes=64)
-        w2_sc_all = keep.tile([P, N], U8, name="w2_sc", align_bytes=64)
-        w2_codes = [w2_codes_all[:, m * P : (m + 1) * P] for m in range(2)]
-        w2_sc = [w2_sc_all[:, m * P : (m + 1) * P] for m in range(2)]
+        w2_codes = mid.tile([P, N], U32, name="w2_codes", align_bytes=64, offset=0)
+        w2_sc = keep.tile([P, N], U8, name="w2_sc", align_bytes=64)
+        w2_first = keep.tile([P, P, PACK], BF16, name="w2_first", align_bytes=64)
+        w2_bf = [w2_first[:], shared_bf[:, 0:P, :]]
+        rr_codes = [mid.tile([P, HALF], U32, name="rr_codes0", align_bytes=64, offset=KIB), keep.tile([P, HALF], U32, name="rr_codes1", align_bytes=64)]
+        rr_sc = [keep.tile([P, HALF], U8, name="rr_sc%d" % h, align_bytes=64) for h in range(2)]
 
-        def weave_views(c0, c1):
-            h, lo, hi = c0 // HALF, c0 % HALF, c0 % HALF + c1 - c0
-            return (rr_bf[h][:, lo:hi, :].rearrange("p (c i) t -> p c t i", i=4), rr_pl[h][:, :, lo:hi].rearrange("p t (c i) -> p c t i", i=4))
+        def weave_views(h, lo, hi):
+            return (woven[h, lo, hi].rearrange("p (c i) t -> p c t i", i=4), rr_pl[h][:, :, lo:hi].rearrange("p t (c i) -> p c t i", i=4))
 
-        def rr_quant(c0, c1):
-            h, lo, hi = c0 // HALF, c0 % HALF, c0 % HALF + c1 - c0
-            nc.vector.quantize_mx(out=rr_codes[:, c0:c1].bitcast(FP8X4), scales=rr_sc[:, c0:c1], in_=rr_bf[h][:, lo:hi, :].rearrange("p c t -> p (c t)"))
+        def rr_quant(h, lo, hi):
+            nc.vector.quantize_mx(out=rr_codes[h][:, lo:hi].bitcast(FP8X4), scales=rr_sc[h][:, lo:hi], in_=woven[h, lo, hi].rearrange("p c t -> p (c t)"))
 
         def w2_quant(m):
-            nc.vector.quantize_mx(out=w2_codes[m].bitcast(FP8X4), scales=w2_sc[m], in_=w2_bf[m][:].rearrange("p c j -> p (c j)"))
+            nc.vector.quantize_mx(out=w2_codes[:, m * P : (m + 1) * P].bitcast(FP8X4), scales=w2_sc[:, m * P : (m + 1) * P], in_=w2_bf[m].rearrange("p c j -> p (c j)"))
 
-        w2_bf = [keep.tile([P, P, PACK], BF16, name="w2_bf%d" % m, tag="pull1%d" % (1 + 2 * m), align_bytes=64) for m in range(2)]
-
-        def w2_views(m):
-            return (w2_bf[m][:].rearrange("p (c i) j -> p c j i", i=4), w2_raw[m][:].rearrange("p j (c i) -> p c j i", i=4))
-
-        o, i = weave_views(0, P)
-        nc.scalar.copy(o, i)
-        o, i = weave_views(P, HALF)
-        nc.scalar.copy(o, i)
-        o, i = w2_views(0)
-        nc.scalar.activation(o, i, COPY)
-        o, i = w2_views(1)
-        nc.scalar.activation(o, i, COPY)
-        rr_quant(0, P)
-        o, i = weave_views(HALF, S)
-        nc.vector.tensor_copy(o, i)
-        rr_quant(P, HALF)
+        nc.gpsimd.tensor_scalar(w2_bf[0], w2_raw[0].rearrange("p j c -> p c j"), 1.0, 0.0, MULT, ADD)
+        nc.gpsimd.tensor_scalar(w2_bf[1][:, 0:W2_SHARE, :], w2_raw[1][:, :, 0:W2_SHARE].rearrange("p j c -> p c j"), 1.0, 0.0, MULT, ADD)
+        nc.scalar.copy(*weave_views(0, 0, P))
+        nc.scalar.copy(*weave_views(0, P, HALF))
+        nc.scalar.copy(*weave_views(1, 0, P))
         w2_quant(0)
-        for c0 in range(HALF, S, P):
-            rr_quant(c0, c0 + P)
-        w2_quant(1)
+        rr_quant(0, 0, HALF)
+        nc.vector.tensor_copy(*weave_views(1, P, HALF))
+        rr_quant(1, 0, P)
+        rr_quant(1, P, HALF)
+        nc.vector.tensor_copy(w2_bf[1][:, W2_SHARE:P, :].rearrange("p (c i) j -> p c j i", i=4), w2_raw[1][:, :, W2_SHARE:P].rearrange("p j (c i) -> p c j i", i=4))
 
         f_sb = [keep.tile([P, S], F32, name="f_sb%d" % m) for m in range(2)]
-        for m, width in ((0, P), (1, HALF)):
-            for c0 in range(0, S, width):
-                cols = slice(c0, c0 + width)
-                f = psum.tile([P, width], F32, name="acc")
-                nc.tensor.matmul_mx(out=f[:], lhsT=w2_codes[m].bitcast(FP8X4),
-                                    lhsT_scale=w2_sc[m],
-                                    rhs=rr_codes[:, cols].bitcast(FP8X4), rhs_scale=rr_sc[:, cols], start=True, stop=True)
-                nc.scalar.copy(f_sb[m][:, cols], f[:])
-
-        own_ps = [psum_own.tile([P, S], F32, name="own_ps%d" % m) for m in range(2)]
-        turned = [keep.tile([P, N], F32, name="turned%d" % b) for b in range(PACK)]
-        for b in (2, 3, 0, 1):
-            cells = slice(b * P, (b + 1) * P)
-            rows = slice(0 if b >= 2 else P, N)
-            f_turned = psum.tile([P, N], F32, name="acc")
-            nc.tensor.matmul_mx(out=f_turned[:, rows], lhsT=rr_codes[:, cells].bitcast(FP8X4), lhsT_scale=rr_sc[:, cells],
-                                rhs=w2_codes_all[:, rows].bitcast(FP8X4), rhs_scale=w2_sc_all[:, rows], start=True, stop=True)
-            nc.scalar.activation(turned[b][:, rows], f_turned[:, rows], COPY, scale=shut_col[:, b : b + 1])
-        for m, b in [(0, 2), (0, 3), (1, 2), (1, 3), (1, 0), (1, 1)]:
-            nc.tensor.transpose(own_ps[m][:, b * P : (b + 1) * P], turned[b][:, m * P : (m + 1) * P], ident[:])
-
         own_sb = keep.tile([P, HALF], F32, name="own_sb")
+        own_ps = [psum_own.tile([P, S], F32, name="own_ps%d" % m) for m in range(2)]
+        pieces = {0: [(0, 0, HALF), (1, 0, P), (1, P, HALF)], 1: [(0, 0, HALF), (1, 0, HALF)]}
+        blocks = {0: (2, 3), 1: (0, 1, 2, 3)}
+        turned = {}
+        for m in range(2):
+            rows = slice(m * P, (m + 1) * P)
+            for h, lo, hi in pieces[m]:
+                f = psum.tile([P, hi - lo], F32, name="acc")
+                nc.tensor.matmul_mx(out=f[:], lhsT=w2_codes[:, rows].bitcast(FP8X4), lhsT_scale=w2_sc[:, rows],
+                                    rhs=rr_codes[h][:, lo:hi].bitcast(FP8X4), rhs_scale=rr_sc[h][:, lo:hi], start=True, stop=True)
+                nc.scalar.copy(f_sb[m][:, h * HALF + lo : h * HALF + hi], f[:])
+            if m == 0:
+                nc.vector.tensor_tensor(own_sb[:], f_sb[0][:, 0:HALF], shut_sb, MULT)
+                w2_quant(1)
+            for b in blocks[m]:
+                cells = slice((b % 2) * P, (b % 2 + 1) * P)
+                f_turned = psum.tile([P, P], F32, name="acc")
+                nc.tensor.matmul_mx(out=f_turned[:], lhsT=rr_codes[b // 2][:, cells].bitcast(FP8X4), lhsT_scale=rr_sc[b // 2][:, cells],
+                                    rhs=w2_codes[:, rows].bitcast(FP8X4), rhs_scale=w2_sc[:, rows], start=True, stop=True)
+                turned[m, b] = keep.tile([P, P], F32, name="turned%d%d" % (m, b))
+                nc.scalar.activation(turned[m, b][:], f_turned[:], COPY, scale=shut_col[:, b : b + 1])
+        for m in range(2):
+            for b in blocks[m]:
+                nc.tensor.transpose(own_ps[m][:, b * P : (b + 1) * P], turned[m, b][:], ident[:])
+
         own = {(m, h): own_ps[m][:, h * HALF : (h + 1) * HALF] for m in range(2) for h in range(2)}
         own[0, 0] = own_sb[:]
-
         got = {(m, h): keep.tile([P, HALF], F32, name="got%d%d" % (m, h)) for m in range(2) for h in range(2)}
 
         def fetch(m, h):
-            cols = slice(h * HALF, (h + 1) * HALF)
-            nc.vector.tensor_tensor(got[m, h][:], f_sb[m][:].indirect(src_sb[:, h * LIST_COLS : (h + 1) * LIST_COLS]), thru_sb[:, cols], MULT)
+            nc.vector.tensor_tensor(got[m, h][:], f_sb[m][:].indirect(src_sb[:, h * LIST_COLS : (h + 1) * LIST_COLS]), thru_sb[:, h * HALF : (h + 1) * HALF], MULT)
 
         def finish(m, h):
-            cols = slice(h * HALF, (h + 1) * HALF)
             res = keep.tile([P, HALF], F32, name="res%d%d" % (m, h))
             nc.vector.tensor_tensor(res[:], got[m, h][:], own[m, h], ADD)
-            nc.sync.dma_start(out[m * P : (m + 1) * P, cols], res[:])
+            nc.sync.dma_start(out[m * P : (m + 1) * P, h * HALF : (h + 1) * HALF], res[:])
 
-        nc.vector.tensor_tensor(own_sb[:], f_sb[0][:, 0:HALF], shut_sb[:], MULT)
         fetch(0, 0)
         fetch(0, 1)
         finish(0, 0)

@@ -21,7 +21,6 @@ P = 128
 PACK = 4
 HALF = S // 2
 LIST_COLS = HALF // 16
-W2_SHARE = 64
 KIB = 1024
 
 
@@ -100,9 +99,9 @@ def tile_picked_ylbm_part_p_kernel(tc, x_words, x_scales, w1, w2, eq, rate, thru
 
         rr_pl = [keep.tile([P, PACK, HALF], BF16, name="rr_pl%d" % h, align_bytes=64) for h in range(2)]
         rr_bf = [keep.tile([P, HALF, PACK], BF16, name="rr_bf0", align_bytes=64)]
-        shared_bf = keep.tile([P, W2_SHARE + P, PACK], BF16, name="shared_bf", align_bytes=64)
+        shared_bf = keep.tile([P, P, PACK], BF16, name="shared_bf", align_bytes=64)
         rr_bf3 = keep.tile([P, P, PACK], BF16, name="rr_bf3", align_bytes=64)
-        woven = {(0, 0, P): rr_bf[0][:, 0:P, :], (0, P, HALF): rr_bf[0][:, P:HALF, :], (0, 0, HALF): rr_bf[0][:], (1, 0, P): shared_bf[:, W2_SHARE : W2_SHARE + P, :], (1, P, HALF): rr_bf3[:]}
+        woven = {(0, 0, P): rr_bf[0][:, 0:P, :], (0, P, HALF): rr_bf[0][:, P:HALF, :], (0, 0, HALF): rr_bf[0][:], (1, 0, P): shared_bf[:], (1, P, HALF): rr_bf3[:]}
         for h in range(2):
             by_quarters = []
             for t in range(PACK):
@@ -129,7 +128,7 @@ def tile_picked_ylbm_part_p_kernel(tc, x_words, x_scales, w1, w2, eq, rate, thru
         w2_codes = mid.tile([P, N], U32, name="w2_codes", align_bytes=64, offset=0)
         w2_sc = keep.tile([P, N], U8, name="w2_sc", align_bytes=64)
         w2_first = keep.tile([P, P, PACK], BF16, name="w2_first", align_bytes=64)
-        w2_bf = [w2_first[:], shared_bf[:, 0:P, :]]
+        w2_bf = [w2_first[:], shared_bf[:]]
         rr_codes = [mid.tile([P, HALF], U32, name="rr_codes0", align_bytes=64, offset=KIB), keep.tile([P, HALF], U32, name="rr_codes1", align_bytes=64)]
         rr_sc = [keep.tile([P, HALF], U8, name="rr_sc%d" % h, align_bytes=64) for h in range(2)]
 
@@ -143,7 +142,6 @@ def tile_picked_ylbm_part_p_kernel(tc, x_words, x_scales, w1, w2, eq, rate, thru
             nc.vector.quantize_mx(out=w2_codes[:, m * P : (m + 1) * P].bitcast(FP8X4), scales=w2_sc[:, m * P : (m + 1) * P], in_=w2_bf[m].rearrange("p c j -> p (c j)"))
 
         nc.gpsimd.tensor_scalar(w2_bf[0], w2_raw[0].rearrange("p j c -> p c j"), 1.0, 0.0, MULT, ADD)
-        nc.gpsimd.tensor_scalar(w2_bf[1][:, 0:W2_SHARE, :], w2_raw[1][:, :, 0:W2_SHARE].rearrange("p j c -> p c j"), 1.0, 0.0, MULT, ADD)
         nc.scalar.copy(*weave_views(0, 0, P))
         nc.scalar.copy(*weave_views(0, P, HALF))
         nc.scalar.copy(*weave_views(1, 0, P))
@@ -152,7 +150,7 @@ def tile_picked_ylbm_part_p_kernel(tc, x_words, x_scales, w1, w2, eq, rate, thru
         nc.vector.tensor_copy(*weave_views(1, P, HALF))
         rr_quant(1, 0, P)
         rr_quant(1, P, HALF)
-        nc.vector.tensor_copy(w2_bf[1][:, W2_SHARE:P, :].rearrange("p (c i) j -> p c j i", i=4), w2_raw[1][:, :, W2_SHARE:P].rearrange("p j (c i) -> p c j i", i=4))
+        nc.vector.tensor_copy(w2_bf[1].rearrange("p (c i) j -> p c j i", i=4), w2_raw[1].rearrange("p j (c i) -> p c j i", i=4))
 
         f_sb = [keep.tile([P, S], F32, name="f_sb%d" % m) for m in range(2)]
         own_sb = keep.tile([P, HALF], F32, name="own_sb")

@@ -60,7 +60,8 @@ def tile_picked_ylbm_part_p_kernel(tc, x_words, x_scales, w1, w2, eq, rate, thru
         late = keep.tile([P, 8 * S], F32, name="late", align_bytes=64)
         eq_sb = {(h, e): late[:, (2 * h + e) * S : (2 * h + e + 1) * S].rearrange("p (t c) -> p t c", t=2) for h in range(2) for e in range(2)}
         eq_pl = {(t, h): late[:, (4 * h + t) * HALF : (4 * h + t + 1) * HALF] for t in range(PACK) for h in range(2)}
-        w2_raw = [late[:, (4 + m) * S : (5 + m) * S].rearrange("p (j c) -> p j c", j=PACK) for m in range(2)]
+        w2_raw_first = keep.tile([P, PACK, P], F32, name="w2_raw_first", tag="w2_raw_first", align_bytes=64)
+        w2_raw = [w2_raw_first[:], late[:, 5 * S : 6 * S].rearrange("p (j c) -> p j c", j=PACK)]
         thru_sb = late[:, 6 * S : 7 * S]
         shut_sb = late[:, 7 * S : 7 * S + HALF]
         shut_col = late[:, 7 * S + HALF : 7 * S + HALF + PACK]
@@ -97,11 +98,10 @@ def tile_picked_ylbm_part_p_kernel(tc, x_words, x_scales, w1, w2, eq, rate, thru
         for h in range(2):
             nc.vector.tensor_copy(xw_g[h][:], xw[:].indirect(offs_sb[:, h * LIST_COLS : (h + 1) * LIST_COLS]))
 
-        rr_pl = [keep.tile([P, PACK, HALF], BF16, name="rr_pl%d" % h, align_bytes=64) for h in range(2)]
+        rr_pl = [keep.tile([P, PACK, HALF], BF16, name="rr_pl%d" % h, tag="planes%d" % h, align_bytes=64) for h in range(2)]
         rr_bf = [keep.tile([P, HALF, PACK], BF16, name="rr_bf0", align_bytes=64)]
-        shared_bf = keep.tile([P, P, PACK], BF16, name="shared_bf", align_bytes=64)
-        rr_bf3 = keep.tile([P, P, PACK], BF16, name="rr_bf3", align_bytes=64)
-        woven = {(0, 0, P): rr_bf[0][:, 0:P, :], (0, P, HALF): rr_bf[0][:, P:HALF, :], (0, 0, HALF): rr_bf[0][:], (1, 0, P): shared_bf[:], (1, P, HALF): rr_bf3[:]}
+        rr_bf2 = keep.tile([P, P, PACK], BF16, name="rr_bf2", align_bytes=64)
+        woven = {(0, 0, HALF): rr_bf[0][:], (1, 0, P): rr_bf2[:]}
         for h in range(2):
             by_quarters = []
             for t in range(PACK):
@@ -117,7 +117,7 @@ def tile_picked_ylbm_part_p_kernel(tc, x_words, x_scales, w1, w2, eq, rate, thru
                 nc.tensor.matmul_mx(out=y[:], lhsT=w1_codes[:, t * P : (t + 1) * P].bitcast(FP8X4), lhsT_scale=w1_sc[t // 2][:, (t % 2) * P : (t % 2 + 1) * P],
                                     rhs=xw_g[h][:].bitcast(FP8X4), rhs_scale=xs_g[:, h * HALF : (h + 1) * HALF],
                                     start=True, stop=True)
-                if t < 2:
+                if h == 0 or t < 2:
                     nc.vector.scalar_tensor_tensor(rr_pl[h][:, t, :], y[:], keep_sb[:, t : t + 1], pull[:], MULT, ADD)
                 else:
                     by_quarters.append((t, y, pull))
@@ -128,8 +128,8 @@ def tile_picked_ylbm_part_p_kernel(tc, x_words, x_scales, w1, w2, eq, rate, thru
         w2_codes = mid.tile([P, N], U32, name="w2_codes", align_bytes=64, offset=0)
         w2_sc = keep.tile([P, N], U8, name="w2_sc", align_bytes=64)
         w2_first = keep.tile([P, P, PACK], BF16, name="w2_first", align_bytes=64)
-        w2_bf = [w2_first[:], shared_bf[:]]
-        rr_codes = [mid.tile([P, HALF], U32, name="rr_codes0", align_bytes=64, offset=KIB), keep.tile([P, HALF], U32, name="rr_codes1", align_bytes=64)]
+        w2_bf = [w2_first[:]]
+        rr_codes = [mid.tile([P, HALF], U32, name="rr_codes0", align_bytes=64, offset=KIB)]
         rr_sc = [keep.tile([P, HALF], U8, name="rr_sc%d" % h, align_bytes=64) for h in range(2)]
 
         def weave_views(h, lo, hi):
@@ -142,20 +142,24 @@ def tile_picked_ylbm_part_p_kernel(tc, x_words, x_scales, w1, w2, eq, rate, thru
             nc.vector.quantize_mx(out=w2_codes[:, m * P : (m + 1) * P].bitcast(FP8X4), scales=w2_sc[:, m * P : (m + 1) * P], in_=w2_bf[m].rearrange("p c j -> p (c j)"))
 
         nc.gpsimd.tensor_scalar(w2_bf[0], w2_raw[0].rearrange("p j c -> p c j"), 1.0, 0.0, MULT, ADD)
-        nc.scalar.copy(*weave_views(0, 0, P))
-        nc.scalar.copy(*weave_views(0, P, HALF))
+        nc.scalar.copy(*weave_views(0, 0, HALF))
         nc.scalar.copy(*weave_views(1, 0, P))
         w2_quant(0)
-        rr_quant(0, 0, HALF)
+        rr_bf3 = keep.tile([P, P, PACK], BF16, name="rr_bf3", tag="w2_raw_first", align_bytes=64)
+        woven[1, P, HALF] = rr_bf3[:]
         nc.vector.tensor_copy(*weave_views(1, P, HALF))
-        rr_quant(1, 0, P)
+        rr_quant(0, 0, HALF)
+        rr_codes.append(keep.tile([P, HALF], U32, name="rr_codes1", tag="planes0", align_bytes=64))
         rr_quant(1, P, HALF)
+        rr_quant(1, 0, P)
+        w2_second = keep.tile([P, P, PACK], BF16, name="w2_second", tag="planes1", align_bytes=64)
+        w2_bf.append(w2_second[:])
         nc.vector.tensor_copy(w2_bf[1].rearrange("p (c i) j -> p c j i", i=4), w2_raw[1].rearrange("p j (c i) -> p c j i", i=4))
 
         f_sb = [keep.tile([P, S], F32, name="f_sb%d" % m) for m in range(2)]
         own_sb = keep.tile([P, HALF], F32, name="own_sb")
         own_ps = [psum_own.tile([P, S], F32, name="own_ps%d" % m) for m in range(2)]
-        pieces = {0: [(0, 0, HALF), (1, 0, P), (1, P, HALF)], 1: [(0, 0, HALF), (1, 0, HALF)]}
+        pieces = {0: [(0, 0, HALF), (1, P, HALF), (1, 0, P)], 1: [(0, 0, HALF), (1, 0, HALF)]}
         blocks = {0: (2, 3), 1: (0, 1, 2, 3)}
         turned = {}
         for m in range(2):

@@ -30,8 +30,10 @@ def tile_picked_ylbm_part_p_kernel(tc, x_words, x_scales, w1, w2, eq, rate, thru
         keep = ctx.enter_context(tc.tile_pool(name="keep", bufs=1))
         head = ctx.enter_context(tc.tile_pool(name="head", bufs=1))
         mid = ctx.enter_context(tc.tile_pool(name="mid", bufs=1))
-        psum = ctx.enter_context(tc.psum_pool(name="psum", bufs=6))
-        psum_own = ctx.enter_context(tc.psum_pool(name="psum_own", bufs=1))
+        psum = ctx.enter_context(tc.psum_pool(name="psum", bufs=1))
+
+        def bank(b, width, name):
+            return psum.tile([P, width], F32, name=name, tag="bank%d" % b)
 
         offs_sb = keep.tile([P, S // 16], U16, name="offs_sb")
         src_sb = keep.tile([P, S // 16], U16, name="src_sb")
@@ -57,26 +59,21 @@ def tile_picked_ylbm_part_p_kernel(tc, x_words, x_scales, w1, w2, eq, rate, thru
         nc.sync.dma_start(xw[:].bitcast(I32), x_words[0].rearrange("p c r -> p (c r)").bitcast(I32))
         nc.sync.dma_start(rate_sb[:], rate.rearrange("(p t) o -> p (t o)", t=PACK))
 
-        late = keep.tile([P, 8 * S], F32, name="late", align_bytes=64)
-        eq_sb = {(h, e): late[:, (2 * h + e) * S : (2 * h + e + 1) * S].rearrange("p (t c) -> p t c", t=2) for h in range(2) for e in range(2)}
-        eq_pl = {(t, h): late[:, (4 * h + t) * HALF : (4 * h + t + 1) * HALF] for t in range(PACK) for h in range(2)}
-        w2_raw_first = keep.tile([P, PACK, P], F32, name="w2_raw_first", tag="w2_raw_first", align_bytes=64)
-        w2_raw = [w2_raw_first[:], late[:, 5 * S : 6 * S].rearrange("p (j c) -> p j c", j=PACK)]
-        thru_sb = late[:, 6 * S : 7 * S]
-        shut_sb = late[:, 7 * S : 7 * S + HALF]
-        shut_col = late[:, 7 * S + HALF : 7 * S + HALF + PACK]
+        eq_sb = {(h, e): mid.tile([P, 2, HALF], F32, name="eq%d%d" % (h, e), align_bytes=64, offset=(2 * h + e) * 2 * KIB) for h in range(2) for e in range(2)}
         eq_rows = eq.rearrange("(p t) c -> p t c", t=PACK)
         for h in range(2):
             for e in range(2):
-                nc.sync.dma_start(eq_sb[h, e], eq_rows[:, 2 * e : 2 * e + 2, h * HALF : (h + 1) * HALF])
-        w2_rows = w2.rearrange("(p j) c -> p j c", j=PACK)
-        for m in range(2):
-            nc.sync.dma_start(w2_raw[m], w2_rows[:, :, m * P : (m + 1) * P])
+                nc.sync.dma_start(eq_sb[h, e][:], eq_rows[:, 2 * e : 2 * e + 2, h * HALF : (h + 1) * HALF])
+        w2_raw = keep.tile([P, PACK, N], F32, name="w2_raw", align_bytes=64)
+        nc.sync.dma_start(w2_raw[:], w2.rearrange("(p j) c -> p j c", j=PACK))
+        thru_sb = keep.tile([P, S], F32, name="thru_sb", align_bytes=64)
+        shut_sb = keep.tile([P, HALF], F32, name="shut_sb", align_bytes=64)
+        shut_col = keep.tile([P, PACK], F32, name="shut_col")
         nc.sync.dma_start(src_sb[:], src)
-        nc.sync.dma_start(shut_sb, shut[:, 0:HALF])
-        nc.sync.dma_start(thru_sb, thru)
+        nc.sync.dma_start(shut_sb[:], shut[:, 0:HALF])
+        nc.sync.dma_start(thru_sb[:], thru)
         with nc.allow_non_contiguous_dma(reason="one value of shut to a partition"):
-            nc.sync.dma_start(shut_col, shut[0, :].rearrange("(b p) -> p b", p=P))
+            nc.sync.dma_start(shut_col[:], shut[0, :].rearrange("(b p) -> p b", p=P))
 
         w1_bf = [keep.tile([P, 2, P, PACK], BF16, name="w1_bf%d" % u, align_bytes=64) for u in range(2)]
         w1_sc = [keep.tile([P, 2 * P], U8, name="w1_sc%d" % u, align_bytes=64) for u in range(2)]
@@ -98,22 +95,17 @@ def tile_picked_ylbm_part_p_kernel(tc, x_words, x_scales, w1, w2, eq, rate, thru
         for h in range(2):
             nc.vector.tensor_copy(xw_g[h][:], xw[:].indirect(offs_sb[:, h * LIST_COLS : (h + 1) * LIST_COLS]))
 
-        rr_pl = [keep.tile([P, PACK, HALF], BF16, name="rr_pl%d" % h, tag="planes%d" % h, align_bytes=64) for h in range(2)]
-        rr_bf = [keep.tile([P, HALF, PACK], BF16, name="rr_bf0", align_bytes=64)]
-        rr_bf2 = keep.tile([P, P, PACK], BF16, name="rr_bf2", align_bytes=64)
-        woven = {(0, 0, HALF): rr_bf[0][:], (1, 0, P): rr_bf2[:]}
+        rr_pl = [keep.tile([P, PACK, HALF], BF16, name="rr_pl%d" % h, align_bytes=64) for h in range(2)]
         for h in range(2):
             by_quarters = []
             for t in range(PACK):
-                if (h, t) == (1, 2):
-                    pull = mid.tile([P, HALF], F32, name="pull12", align_bytes=64, offset=KIB // 2)
+                pull = keep.tile([P, HALF], F32, name="pull%d%d" % (h, t), tag="pull%d%d" % (h, t), align_bytes=64)
+                plane = eq_sb[h, t // 2][:, t % 2, :]
+                if PACK * h + t > PACK:
+                    nc.gpsimd.tensor_scalar(pull[:], plane, rate_sb[:, t : t + 1], 0.0, MULT, ADD)
                 else:
-                    pull = keep.tile([P, HALF], F32, name="pull%d%d" % (h, t), tag="pull%d%d" % (h, t), align_bytes=64)
-                if h == 1 and t < 2:
-                    nc.gpsimd.tensor_scalar(pull[:], eq_pl[t, h], rate_sb[:, t : t + 1], 0.0, MULT, ADD)
-                else:
-                    nc.scalar.activation(pull[:], eq_pl[t, h], COPY, scale=rate_sb[:, t : t + 1])
-                y = psum.tile([P, HALF], F32, name="acc")
+                    nc.scalar.activation(pull[:], plane, COPY, scale=rate_sb[:, t : t + 1])
+                y = bank(PACK * h + t, HALF, "y%d%d" % (h, t))
                 nc.tensor.matmul_mx(out=y[:], lhsT=w1_codes[:, t * P : (t + 1) * P].bitcast(FP8X4), lhsT_scale=w1_sc[t // 2][:, (t % 2) * P : (t % 2 + 1) * P],
                                     rhs=xw_g[h][:].bitcast(FP8X4), rhs_scale=xs_g[:, h * HALF : (h + 1) * HALF],
                                     start=True, stop=True)
@@ -125,66 +117,65 @@ def tile_picked_ylbm_part_p_kernel(tc, x_words, x_scales, w1, w2, eq, rate, thru
                 for t, y, pull in by_quarters:
                     nc.vector.scalar_tensor_tensor(rr_pl[h][:, t, c0 : c0 + P], y[:, c0 : c0 + P], keep_sb[:, t : t + 1], pull[:, c0 : c0 + P], MULT, ADD)
 
-        w2_codes = mid.tile([P, N], U32, name="w2_codes", align_bytes=64, offset=0)
-        w2_sc = keep.tile([P, N], U8, name="w2_sc", align_bytes=64)
-        w2_first = keep.tile([P, P, PACK], BF16, name="w2_first", align_bytes=64)
-        w2_bf = [w2_first[:]]
-        rr_codes = [mid.tile([P, HALF], U32, name="rr_codes0", align_bytes=64, offset=KIB)]
+        pieces = [(0, 0, HALF), (1, 0, P), (1, P, HALF)]
+        woven = {key: keep.tile([P, key[2] - key[1], PACK], BF16, name="woven%d%d" % key[:2], align_bytes=64) for key in pieces}
+        rr_codes = [mid.tile([P, HALF], U32, name="rr_codes0", align_bytes=64, offset=6 * KIB), keep.tile([P, HALF], U32, name="rr_codes1", align_bytes=64)]
         rr_sc = [keep.tile([P, HALF], U8, name="rr_sc%d" % h, align_bytes=64) for h in range(2)]
+        w2_bf = [mid.tile([P, P, PACK], BF16, name="w2_bf0", align_bytes=64, offset=7 * KIB), keep.tile([P, P, PACK], BF16, name="w2_bf1", tag="pull13", align_bytes=64)]
+        w2_codes = keep.tile([P, N], U32, name="w2_codes", align_bytes=64)
+        w2_sc = keep.tile([P, N], U8, name="w2_sc", align_bytes=64)
 
         def weave_views(h, lo, hi):
-            return (woven[h, lo, hi].rearrange("p (c i) t -> p c t i", i=4), rr_pl[h][:, :, lo:hi].rearrange("p t (c i) -> p c t i", i=4))
+            return (woven[h, lo, hi][:].rearrange("p (c i) t -> p c t i", i=4), rr_pl[h][:, :, lo:hi].rearrange("p t (c i) -> p c t i", i=4))
+
+        def w2_views(m):
+            return (w2_bf[m][:].rearrange("p (c i) j -> p c j i", i=4), w2_raw[:, :, m * P : (m + 1) * P].rearrange("p j (c i) -> p c j i", i=4))
 
         def rr_quant(h, lo, hi):
-            nc.vector.quantize_mx(out=rr_codes[h][:, lo:hi].bitcast(FP8X4), scales=rr_sc[h][:, lo:hi], in_=woven[h, lo, hi].rearrange("p c t -> p (c t)"))
+            nc.vector.quantize_mx(out=rr_codes[h][:, lo:hi].bitcast(FP8X4), scales=rr_sc[h][:, lo:hi], in_=woven[h, lo, hi][:].rearrange("p c t -> p (c t)"))
 
         def w2_quant(m):
-            nc.vector.quantize_mx(out=w2_codes[:, m * P : (m + 1) * P].bitcast(FP8X4), scales=w2_sc[:, m * P : (m + 1) * P], in_=w2_bf[m].rearrange("p c j -> p (c j)"))
+            nc.vector.quantize_mx(out=w2_codes[:, m * P : (m + 1) * P].bitcast(FP8X4), scales=w2_sc[:, m * P : (m + 1) * P], in_=w2_bf[m][:].rearrange("p c j -> p (c j)"))
 
-        nc.gpsimd.tensor_scalar(w2_bf[0], w2_raw[0].rearrange("p j c -> p c j"), 1.0, 0.0, MULT, ADD)
-        nc.scalar.copy(*weave_views(0, 0, HALF))
-        nc.scalar.copy(*weave_views(1, 0, P))
+        nc.scalar.copy(*weave_views(*pieces[0]))
+        nc.scalar.copy(*weave_views(*pieces[1]))
+        rr_quant(*pieces[0])
+        nc.vector.tensor_copy(*w2_views(0))
+        nc.vector.tensor_copy(*weave_views(*pieces[2]))
+        nc.scalar.copy(*w2_views(1))
         w2_quant(0)
-        rr_bf3 = keep.tile([P, P, PACK], BF16, name="rr_bf3", tag="w2_raw_first", align_bytes=64)
-        woven[1, P, HALF] = rr_bf3[:]
-        nc.vector.tensor_copy(*weave_views(1, P, HALF))
-        rr_quant(0, 0, HALF)
-        rr_codes.append(keep.tile([P, HALF], U32, name="rr_codes1", tag="planes0", align_bytes=64))
-        rr_quant(1, P, HALF)
-        rr_quant(1, 0, P)
-        w2_second = keep.tile([P, P, PACK], BF16, name="w2_second", tag="planes1", align_bytes=64)
-        w2_bf.append(w2_second[:])
-        nc.vector.tensor_copy(w2_bf[1].rearrange("p (c i) j -> p c j i", i=4), w2_raw[1].rearrange("p j (c i) -> p c j i", i=4))
+        rr_quant(*pieces[1])
+        rr_quant(*pieces[2])
+        w2_quant(1)
 
         f_sb = [keep.tile([P, S], F32, name="f_sb%d" % m) for m in range(2)]
         own_sb = keep.tile([P, HALF], F32, name="own_sb")
-        own_ps = [psum_own.tile([P, S], F32, name="own_ps%d" % m) for m in range(2)]
-        pieces = {0: [(0, 0, HALF), (1, P, HALF), (1, 0, P)], 1: [(0, 0, HALF), (1, 0, HALF)]}
-        blocks = {0: (2, 3), 1: (0, 1, 2, 3)}
-        turned = {}
-        for m in range(2):
+        f_pieces = [(0,) + key for key in pieces] + [(1, h, 0, HALF) for h in range(2)]
+        for b, (m, h, lo, hi) in enumerate(f_pieces):
             rows = slice(m * P, (m + 1) * P)
-            for h, lo, hi in pieces[m]:
-                f = psum.tile([P, hi - lo], F32, name="acc")
-                nc.tensor.matmul_mx(out=f[:], lhsT=w2_codes[:, rows].bitcast(FP8X4), lhsT_scale=w2_sc[:, rows],
-                                    rhs=rr_codes[h][:, lo:hi].bitcast(FP8X4), rhs_scale=rr_sc[h][:, lo:hi], start=True, stop=True)
-                nc.scalar.copy(f_sb[m][:, h * HALF + lo : h * HALF + hi], f[:])
-            if m == 0:
-                nc.vector.tensor_tensor(own_sb[:], f_sb[0][:, 0:HALF], shut_sb, MULT)
-                w2_quant(1)
-            for b in blocks[m]:
-                cells = slice((b % 2) * P, (b % 2 + 1) * P)
-                f_turned = psum.tile([P, P], F32, name="acc")
-                nc.tensor.matmul_mx(out=f_turned[:], lhsT=rr_codes[b // 2][:, cells].bitcast(FP8X4), lhsT_scale=rr_sc[b // 2][:, cells],
-                                    rhs=w2_codes[:, rows].bitcast(FP8X4), rhs_scale=w2_sc[:, rows], start=True, stop=True)
-                turned[m, b] = keep.tile([P, P], F32, name="turned%d%d" % (m, b))
-                nc.scalar.activation(turned[m, b][:], f_turned[:], COPY, scale=shut_col[:, b : b + 1])
-        for m in range(2):
-            for b in blocks[m]:
-                nc.tensor.transpose(own_ps[m][:, b * P : (b + 1) * P], turned[m, b][:], ident[:])
+            f = bank(b, hi - lo, "f%d" % b)
+            nc.tensor.matmul_mx(out=f[:], lhsT=w2_codes[:, rows].bitcast(FP8X4), lhsT_scale=w2_sc[:, rows],
+                                rhs=rr_codes[h][:, lo:hi].bitcast(FP8X4), rhs_scale=rr_sc[h][:, lo:hi], start=True, stop=True)
+            nc.scalar.copy(f_sb[m][:, h * HALF + lo : h * HALF + hi], f[:])
+        nc.vector.tensor_tensor(own_sb[:], f_sb[0][:, 0:HALF], shut_sb[:], MULT)
 
-        own = {(m, h): own_ps[m][:, h * HALF : (h + 1) * HALF] for m in range(2) for h in range(2)}
-        own[0, 0] = own_sb[:]
+        turned = {}
+        for b, rows, bk in ((2, slice(0, N), 5), (3, slice(0, N), 6), (0, slice(P, N), 7), (1, slice(P, N), 0)):
+            cells = slice((b % 2) * P, (b % 2 + 1) * P)
+            width = rows.stop - rows.start
+            f_turned = bank(bk, width, "f_turned%d" % b)
+            nc.tensor.matmul_mx(out=f_turned[:], lhsT=rr_codes[b // 2][:, cells].bitcast(FP8X4), lhsT_scale=rr_sc[b // 2][:, cells],
+                                rhs=w2_codes[:, rows].bitcast(FP8X4), rhs_scale=w2_sc[:, rows], start=True, stop=True)
+            scaled = keep.tile([P, width], F32, name="turned%d" % b)
+            nc.scalar.activation(scaled[:], f_turned[:], COPY, scale=shut_col[:, b : b + 1])
+            for r0 in range(rows.start, rows.stop, P):
+                turned[r0 // P, b] = scaled[:, r0 - rows.start : r0 - rows.start + P]
+        own = {(0, 0): own_sb}
+        for m, h, bk in ((0, 1, 1), (1, 1, 2), (1, 0, 3)):
+            own[m, h] = bank(bk, HALF, "own%d%d" % (m, h))
+            for c in range(2):
+                nc.tensor.transpose(own[m, h][:, c * P : (c + 1) * P], turned[m, 2 * h + c], ident[:])
+
         got = {(m, h): keep.tile([P, HALF], F32, name="got%d%d" % (m, h)) for m in range(2) for h in range(2)}
 
         def fetch(m, h):
@@ -192,14 +183,14 @@ def tile_picked_ylbm_part_p_kernel(tc, x_words, x_scales, w1, w2, eq, rate, thru
 
         def finish(m, h):
             res = keep.tile([P, HALF], F32, name="res%d%d" % (m, h))
-            nc.vector.tensor_tensor(res[:], got[m, h][:], own[m, h], ADD)
+            nc.vector.tensor_tensor(res[:], got[m, h][:], own[m, h][:], ADD)
             nc.sync.dma_start(out[m * P : (m + 1) * P, h * HALF : (h + 1) * HALF], res[:])
 
         fetch(0, 0)
         fetch(0, 1)
         finish(0, 0)
-        fetch(1, 0)
         fetch(1, 1)
+        fetch(1, 0)
         finish(0, 1)
-        finish(1, 0)
         finish(1, 1)
+        finish(1, 0)

@@ -160,7 +160,10 @@ def tile_picked_ylbm_part_p_kernel(tc, x_words, x_scales, w1, w2, eq, rate, thru
         nc.vector.tensor_tensor(own_sb[:], f_sb[0][:, 0:HALF], shut_sb[:], MULT)
 
         turned = {}
+        plain = keep.tile([P, HALF], F32, name="plain")
         for b, rows, bk in ((2, slice(0, N), 5), (3, slice(0, N), 6), (0, slice(P, N), 7), (1, slice(P, N), 0)):
+            if b == 0:
+                nc.scalar.activation(plain[:], f_sb[1][:].indirect(src_sb[:, 0:LIST_COLS]), COPY)
             cells = slice((b % 2) * P, (b % 2 + 1) * P)
             width = rows.stop - rows.start
             f_turned = bank(bk, width, "f_turned%d" % b)
@@ -190,7 +193,7 @@ def tile_picked_ylbm_part_p_kernel(tc, x_words, x_scales, w1, w2, eq, rate, thru
         fetch(0, 1)
         finish(0, 0)
         fetch(1, 1)
-        fetch(1, 0)
+        nc.gpsimd.tensor_tensor(got[1, 0][:], plain[:], thru_sb[:, 0:HALF], MULT)
         finish(0, 1)
         finish(1, 1)
         finish(1, 0)

@@ -118,7 +118,7 @@ def tile_picked_ylbm_part_p_kernel(tc, x_words, x_scales, w1, w2, eq, rate, thru
                     nc.vector.scalar_tensor_tensor(rr_pl[h][:, t, c0 : c0 + P], y[:, c0 : c0 + P], keep_sb[:, t : t + 1], pull[:, c0 : c0 + P], MULT, ADD)
 
         pieces = [(0, 0, HALF), (1, 0, P), (1, P, HALF)]
-        woven = {key: keep.tile([P, key[2] - key[1], PACK], BF16, name="woven%d%d" % key[:2], align_bytes=64) for key in pieces}
+        woven = {key: keep.tile([P, key[2] - key[1], PACK], BF16, name="woven%d%d" % key[:2], tag="rr_pl0" if key == pieces[2] else "woven%d%d" % key[:2], align_bytes=64) for key in pieces}
         rr_codes = [mid.tile([P, HALF], U32, name="rr_codes0", align_bytes=64, offset=6 * KIB), keep.tile([P, HALF], U32, name="rr_codes1", align_bytes=64)]
         rr_sc = [keep.tile([P, HALF], U8, name="rr_sc%d" % h, align_bytes=64) for h in range(2)]
         w2_bf = [mid.tile([P, P, PACK], BF16, name="w2_bf0", align_bytes=64, offset=7 * KIB), keep.tile([P, P, PACK], BF16, name="w2_bf1", tag="pull13", align_bytes=64)]
@@ -139,11 +139,11 @@ def tile_picked_ylbm_part_p_kernel(tc, x_words, x_scales, w1, w2, eq, rate, thru
 
         nc.scalar.copy(*weave_views(*pieces[0]))
         nc.scalar.copy(*weave_views(*pieces[1]))
-        rr_quant(*pieces[0])
         nc.vector.tensor_copy(*w2_views(0))
+        rr_quant(*pieces[0])
+        w2_quant(0)
         nc.vector.tensor_copy(*weave_views(*pieces[2]))
         nc.scalar.copy(*w2_views(1))
-        w2_quant(0)
         rr_quant(*pieces[1])
         rr_quant(*pieces[2])
         w2_quant(1)

@@ -22,6 +22,7 @@ PACK = 4
 HALF = S // 2
 LIST_COLS = HALF // 16
 KIB = 1024
+ROW = 256
 
 
 def tile_picked_ylbm_part_p_kernel(tc, x_words, x_scales, w1, w2, eq, rate, thru, shut, offs, src, out):
@@ -37,10 +38,10 @@ def tile_picked_ylbm_part_p_kernel(tc, x_words, x_scales, w1, w2, eq, rate, thru
 
         offs_sb = keep.tile([P, S // 16], U16, name="offs_sb")
         src_sb = keep.tile([P, S // 16], U16, name="src_sb")
-        xw = keep.tile([P, T], U32, name="xw", align_bytes=64)
-        xs = head.tile([P, T], U8, name="xs", align_bytes=64, offset=KIB)
+        xw = keep.tile([P, T], U32, name="xw", align_bytes=ROW)
+        xs = head.tile([P, T], U8, name="xs", align_bytes=ROW, offset=KIB)
         xs_g = keep.tile([P, S], U8, name="xs_g", align_bytes=64)
-        w1_raw = [keep.tile([P, 2, H], F32, name="w1_raw%d" % e) for e in range(2)]
+        w1_raw = [keep.tile([P, 2, H], F32, name="w1_raw%d" % e, align_bytes=ROW) for e in range(2)]
         rate_sb = keep.tile([P, PACK], F32, name="rate_sb")
         keep_sb = keep.tile([P, PACK], F32, name="keep_sb")
         ident = keep.tile([P, P], F32, name="ident")
@@ -59,15 +60,15 @@ def tile_picked_ylbm_part_p_kernel(tc, x_words, x_scales, w1, w2, eq, rate, thru
         nc.sync.dma_start(xw[:].bitcast(I32), x_words[0].rearrange("p c r -> p (c r)").bitcast(I32))
         nc.sync.dma_start(rate_sb[:], rate.rearrange("(p t) o -> p (t o)", t=PACK))
 
-        eq_sb = {(h, e): mid.tile([P, 2, HALF], F32, name="eq%d%d" % (h, e), align_bytes=64, offset=(2 * h + e) * 2 * KIB) for h in range(2) for e in range(2)}
+        eq_sb = {(h, e): mid.tile([P, 2, HALF], F32, name="eq%d%d" % (h, e), align_bytes=ROW, offset=(2 * h + e) * 2 * KIB) for h in range(2) for e in range(2)}
         eq_rows = eq.rearrange("(p t) c -> p t c", t=PACK)
         for h in range(2):
             for e in range(2):
                 nc.sync.dma_start(eq_sb[h, e][:], eq_rows[:, 2 * e : 2 * e + 2, h * HALF : (h + 1) * HALF])
-        w2_raw = keep.tile([P, PACK, N], F32, name="w2_raw", align_bytes=64)
+        w2_raw = keep.tile([P, PACK, N], F32, name="w2_raw", align_bytes=ROW)
         nc.sync.dma_start(w2_raw[:], w2.rearrange("(p j) c -> p j c", j=PACK))
-        thru_sb = keep.tile([P, S], F32, name="thru_sb", align_bytes=64)
-        shut_sb = keep.tile([P, HALF], F32, name="shut_sb", align_bytes=64)
+        thru_sb = keep.tile([P, S], F32, name="thru_sb", align_bytes=ROW)
+        shut_sb = keep.tile([P, HALF], F32, name="shut_sb", align_bytes=ROW)
         shut_col = keep.tile([P, PACK], F32, name="shut_col")
         nc.sync.dma_start(src_sb[:], src)
         nc.sync.dma_start(shut_sb[:], shut[:, 0:HALF])
@@ -185,7 +186,7 @@ def tile_picked_ylbm_part_p_kernel(tc, x_words, x_scales, w1, w2, eq, rate, thru
             nc.vector.tensor_tensor(got[m, h][:], f_sb[m][:].indirect(src_sb[:, h * LIST_COLS : (h + 1) * LIST_COLS]), thru_sb[:, h * HALF : (h + 1) * HALF], MULT)
 
         def finish(m, h):
-            res = keep.tile([P, HALF], F32, name="res%d%d" % (m, h))
+            res = keep.tile([P, HALF], F32, name="res%d%d" % (m, h), align_bytes=ROW)
             nc.vector.tensor_tensor(res[:], got[m, h][:], own[m, h][:], ADD)
             nc.sync.dma_start(out[m * P : (m + 1) * P, h * HALF : (h + 1) * HALF], res[:])
 

from contextlib import ExitStack

import concourse.mybir as mybir
from concourse.masks import make_identity

K, T, S, H, N = 512, 2048, 512, 512, 256
FLOPS = 2 * K * H * S + 2 * H * N * S

F32 = mybir.dt.float32
BF16 = mybir.dt.bfloat16
I32 = mybir.dt.int32
U32 = mybir.dt.uint32
U16 = mybir.dt.uint16
U8 = mybir.dt.uint8
FP8X4 = mybir.dt.float8_e4m3fn_x4
MULT = mybir.AluOpType.mult
ADD = mybir.AluOpType.add
COPY = mybir.ActivationFunctionType.Copy

P = 128
PACK = 4
HALF = S // 2
LIST_COLS = HALF // 16
KIB = 1024
ROW = 256


def tile_picked_ylbm_part_p_kernel(tc, x_words, x_scales, w1, w2, eq, rate, thru, shut, offs, src, out):
    nc = tc.nc
    with ExitStack() as ctx:
        keep = ctx.enter_context(tc.tile_pool(name="keep", bufs=1))
        head = ctx.enter_context(tc.tile_pool(name="head", bufs=1))
        mid = ctx.enter_context(tc.tile_pool(name="mid", bufs=1))
        psum = ctx.enter_context(tc.psum_pool(name="psum", bufs=1))

        def bank(b, width, name):
            return psum.tile([P, width], F32, name=name, tag="bank%d" % b)

        offs_sb = keep.tile([P, S // 16], U16, name="offs_sb")
        src_sb = keep.tile([P, S // 16], U16, name="src_sb")
        xw = keep.tile([P, T], U32, name="xw", align_bytes=ROW)
        xs = head.tile([P, T], U8, name="xs", align_bytes=ROW, offset=KIB)
        xs_g = keep.tile([P, S], U8, name="xs_g", align_bytes=64)
        w1_raw = [keep.tile([P, 2, H], F32, name="w1_raw%d" % e, align_bytes=ROW) for e in range(2)]
        rate_sb = keep.tile([P, PACK], F32, name="rate_sb")
        keep_sb = keep.tile([P, PACK], F32, name="keep_sb")
        ident = keep.tile([P, P], F32, name="ident")

        nc.vector.memset(xs[:].bitcast(I32), 0)
        nc.vector.memset(ident[:], 0.0)
        make_identity(nc, ident[:], nomemset=True)

        w1_rows = w1.rearrange("(p j) c -> p j c", j=PACK)
        nc.sync.dma_start(w1_raw[0][:], w1_rows[:, 0:2, :])
        nc.sync.dma_start(offs_sb[:], offs)
        scale_rows = x_scales[0].rearrange("(q r) c -> r q c", r=4)
        for r in range(4):
            nc.sync.dma_start(xs[r:P:32, :].bitcast(I32), scale_rows[r].bitcast(I32))
        nc.sync.dma_start(w1_raw[1][:], w1_rows[:, 2:4, :])
        nc.sync.dma_start(xw[:].bitcast(I32), x_words[0].rearrange("p c r -> p (c r)").bitcast(I32))
        nc.sync.dma_start(rate_sb[:], rate.rearrange("(p t) o -> p (t o)", t=PACK))

        eq_sb = {(h, e): mid.tile([P, 2, HALF], F32, name="eq%d%d" % (h, e), align_bytes=ROW, offset=(2 * h + e) * 2 * KIB) for h in range(2) for e in range(2)}
        eq_rows = eq.rearrange("(p t) c -> p t c", t=PACK)
        for h in range(2):
            for e in range(2):
                nc.sync.dma_start(eq_sb[h, e][:], eq_rows[:, 2 * e : 2 * e + 2, h * HALF : (h + 1) * HALF])
        w2_raw = keep.tile([P, PACK, N], F32, name="w2_raw", align_bytes=ROW)
        nc.sync.dma_start(w2_raw[:], w2.rearrange("(p j) c -> p j c", j=PACK))
        thru_sb = keep.tile([P, S], F32, name="thru_sb", align_bytes=ROW)
        shut_sb = keep.tile([P, HALF], F32, name="shut_sb", align_bytes=ROW)
        shut_col = keep.tile([P, PACK], F32, name="shut_col")
        nc.sync.dma_start(src_sb[:], src)
        nc.sync.dma_start(shut_sb[:], shut[:, 0:HALF])
        nc.sync.dma_start(thru_sb[:], thru)
        with nc.allow_non_contiguous_dma(reason="one value of shut to a partition"):
            nc.sync.dma_start(shut_col[:], shut[0, :].rearrange("(b p) -> p b", p=P))

        w1_bf = [keep.tile([P, 2, P, PACK], BF16, name="w1_bf%d" % u, align_bytes=64) for u in range(2)]
        w1_sc = [keep.tile([P, 2 * P], U8, name="w1_sc%d" % u, align_bytes=64) for u in range(2)]
        w1_codes = head.tile([P, H], U32, name="w1_codes", align_bytes=64, offset=0)

        def w1_views(u, e):
            return (w1_bf[u][:, :, :, 2 * e : 2 * e + 2].rearrange("p t m j -> p m j t"),
                    w1_raw[e][:].rearrange("p j (m t) -> p m j t", t=PACK)[:, :, :, 2 * u : 2 * u + 2])

        for u in range(2):
            nc.scalar.activation(*w1_views(u, 0), COPY)
        nc.vector.tensor_copy(xs_g[:], xs[:].indirect(offs_sb[:]))
        nc.vector.tensor_copy(*w1_views(0, 1))
        nc.scalar.activation(*w1_views(1, 1), COPY)
        for u in range(2):
            nc.vector.quantize_mx(out=w1_codes[:, 2 * u * P : 2 * (u + 1) * P].bitcast(FP8X4), scales=w1_sc[u][:], in_=w1_bf[u][:].rearrange("p t m j -> p (t m j)"))
        nc.scalar.activation(keep_sb[:], rate_sb[:], COPY, scale=-1.0, bias=1.0)
        xw_g = [keep.tile([P, HALF], U32, name="xw_g%d" % h, align_bytes=64) for h in range(2)]
        for h in range(2):
            nc.vector.tensor_copy(xw_g[h][:], xw[:].indirect(offs_sb[:, h * LIST_COLS : (h + 1) * LIST_COLS]))

        rr_pl = [keep.tile([P, PACK, HALF], BF16, name="rr_pl%d" % h, align_bytes=64) for h in range(2)]
        for h in range(2):
            by_quarters = []
            for t in range(PACK):
                pull = keep.tile([P, HALF], F32, name="pull%d%d" % (h, t), tag="pull%d%d" % (h, t), align_bytes=64)
                plane = eq_sb[h, t // 2][:, t % 2, :]
                if PACK * h + t > PACK:
                    nc.gpsimd.tensor_scalar(pull[:], plane, rate_sb[:, t : t + 1], 0.0, MULT, ADD)
                else:
                    nc.scalar.activation(pull[:], plane, COPY, scale=rate_sb[:, t : t + 1])
                y = bank(PACK * h + t, HALF, "y%d%d" % (h, t))
                nc.tensor.matmul_mx(out=y[:], lhsT=w1_codes[:, t * P : (t + 1) * P].bitcast(FP8X4), lhsT_scale=w1_sc[t // 2][:, (t % 2) * P : (t % 2 + 1) * P],
                                    rhs=xw_g[h][:].bitcast(FP8X4), rhs_scale=xs_g[:, h * HALF : (h + 1) * HALF],
                                    start=True, stop=True)
                if h == 0 or t < 2:
                    nc.vector.scalar_tensor_tensor(rr_pl[h][:, t, :], y[:], keep_sb[:, t : t + 1], pull[:], MULT, ADD)
                else:
                    by_quarters.append((t, y, pull))
            for c0 in range(0, HALF, P):
                for t, y, pull in by_quarters:
                    nc.vector.scalar_tensor_tensor(rr_pl[h][:, t, c0 : c0 + P], y[:, c0 : c0 + P], keep_sb[:, t : t + 1], pull[:, c0 : c0 + P], MULT, ADD)

        pieces = [(0, 0, HALF), (1, 0, P), (1, P, HALF)]
        woven = {key: keep.tile([P, key[2] - key[1], PACK], BF16, name="woven%d%d" % key[:2], tag="rr_pl0" if key == pieces[2] else "woven%d%d" % key[:2], align_bytes=64) for key in pieces}
        rr_codes = [mid.tile([P, HALF], U32, name="rr_codes0", align_bytes=64, offset=6 * KIB), keep.tile([P, HALF], U32, name="rr_codes1", align_bytes=64)]
        rr_sc = [keep.tile([P, HALF], U8, name="rr_sc%d" % h, align_bytes=64) for h in range(2)]
        w2_bf = [mid.tile([P, P, PACK], BF16, name="w2_bf0", align_bytes=64, offset=7 * KIB), keep.tile([P, P, PACK], BF16, name="w2_bf1", tag="pull13", align_bytes=64)]
        w2_codes = keep.tile([P, N], U32, name="w2_codes", align_bytes=64)
        w2_sc = keep.tile([P, N], U8, name="w2_sc", align_bytes=64)

        def weave_views(h, lo, hi):
            return (woven[h, lo, hi][:].rearrange("p (c i) t -> p c t i", i=4), rr_pl[h][:, :, lo:hi].rearrange("p t (c i) -> p c t i", i=4))

        def w2_views(m):
            return (w2_bf[m][:].rearrange("p (c i) j -> p c j i", i=4), w2_raw[:, :, m * P : (m + 1) * P].rearrange("p j (c i) -> p c j i", i=4))

        def rr_quant(h, lo, hi):
            nc.vector.quantize_mx(out=rr_codes[h][:, lo:hi].bitcast(FP8X4), scales=rr_sc[h][:, lo:hi], in_=woven[h, lo, hi][:].rearrange("p c t -> p (c t)"))

        def w2_quant(m):
            nc.vector.quantize_mx(out=w2_codes[:, m * P : (m + 1) * P].bitcast(FP8X4), scales=w2_sc[:, m * P : (m + 1) * P], in_=w2_bf[m][:].rearrange("p c j -> p (c j)"))

        nc.scalar.copy(*weave_views(*pieces[0]))
        nc.scalar.copy(*weave_views(*pieces[1]))
        nc.vector.tensor_copy(*w2_views(0))
        rr_quant(*pieces[0])
        w2_quant(0)
        nc.vector.tensor_copy(*weave_views(*pieces[2]))
        nc.scalar.copy(*w2_views(1))
        rr_quant(*pieces[1])
        rr_quant(*pieces[2])
        w2_quant(1)

        f_sb = [keep.tile([P, S], F32, name="f_sb%d" % m) for m in range(2)]
        own_sb = keep.tile([P, HALF], F32, name="own_sb")
        f_pieces = [(0,) + key for key in pieces] + [(1, h, 0, HALF) for h in range(2)]
        for b, (m, h, lo, hi) in enumerate(f_pieces):
            rows = slice(m * P, (m + 1) * P)
            f = bank(b, hi - lo, "f%d" % b)
            nc.tensor.matmul_mx(out=f[:], lhsT=w2_codes[:, rows].bitcast(FP8X4), lhsT_scale=w2_sc[:, rows],
                                rhs=rr_codes[h][:, lo:hi].bitcast(FP8X4), rhs_scale=rr_sc[h][:, lo:hi], start=True, stop=True)
            nc.scalar.copy(f_sb[m][:, h * HALF + lo : h * HALF + hi], f[:])
        nc.vector.tensor_tensor(own_sb[:], f_sb[0][:, 0:HALF], shut_sb[:], MULT)

        turned = {}
        plain = keep.tile([P, HALF], F32, name="plain")
        for b, rows, bk in ((2, slice(0, N), 5), (3, slice(0, N), 6), (0, slice(P, N), 7), (1, slice(P, N), 0)):
            if b == 0:
                nc.scalar.activation(plain[:], f_sb[1][:].indirect(src_sb[:, 0:LIST_COLS]), COPY)
            cells = slice((b % 2) * P, (b % 2 + 1) * P)
            width = rows.stop - rows.start
            f_turned = bank(bk, width, "f_turned%d" % b)
            nc.tensor.matmul_mx(out=f_turned[:], lhsT=rr_codes[b // 2][:, cells].bitcast(FP8X4), lhsT_scale=rr_sc[b // 2][:, cells],
                                rhs=w2_codes[:, rows].bitcast(FP8X4), rhs_scale=w2_sc[:, rows], start=True, stop=True)
            scaled = keep.tile([P, width], F32, name="turned%d" % b)
            nc.scalar.activation(scaled[:], f_turned[:], COPY, scale=shut_col[:, b : b + 1])
            for r0 in range(rows.start, rows.stop, P):
                turned[r0 // P, b] = scaled[:, r0 - rows.start : r0 - rows.start + P]
        own = {(0, 0): own_sb}
        for m, h, bk in ((0, 1, 1), (1, 1, 2), (1, 0, 3)):
            own[m, h] = bank(bk, HALF, "own%d%d" % (m, h))
            for c in range(2):
                nc.tensor.transpose(own[m, h][:, c * P : (c + 1) * P], turned[m, 2 * h + c], ident[:])

        got = {(m, h): keep.tile([P, HALF], F32, name="got%d%d" % (m, h)) for m in range(2) for h in range(2)}

        def fetch(m, h):
            nc.vector.tensor_tensor(got[m, h][:], f_sb[m][:].indirect(src_sb[:, h * LIST_COLS : (h + 1) * LIST_COLS]), thru_sb[:, h * HALF : (h + 1) * HALF], MULT)

        def finish(m, h):
            res = keep.tile([P, HALF], F32, name="res%d%d" % (m, h), align_bytes=ROW)
            nc.vector.tensor_tensor(res[:], got[m, h][:], own[m, h][:], ADD)
            nc.sync.dma_start(out[m * P : (m + 1) * P, h * HALF : (h + 1) * HALF], res[:])

        fetch(0, 0)
        fetch(0, 1)
        finish(0, 0)
        fetch(1, 1)
        nc.gpsimd.tensor_tensor(got[1, 0][:], plain[:], thru_sb[:, 0:HALF], MULT)
        finish(0, 1)
        finish(1, 1)
        finish(1, 0)
